import numpy as np, ml_dtypes
CORES = [40,41,42,43,44,45,46,47]
N = 8
import mx_ref
BF = ml_dtypes.bfloat16
def cols(t, e):
    v = np.concatenate([t.reshape(128, -1, 4), np.zeros((128, 1, 4), BF)], axis=1)
    return np.ascontiguousarray(v[:, e]).reshape(128, -1)
def decode(q):
    o = []
    for b in range(4):
        e = np.zeros((128, 128, 4), np.float32); e[np.arange(128), np.arange(128), b] = 1
        o.append(mx_ref.matmul(mx_ref.quantize(e.reshape(128, 512).astype(BF)), q))
    return np.stack(o, axis=2).reshape(128, -1)
def f(rng, *shape):
    return mx_ref.flush((rng.standard_normal(shape, dtype=np.float32) * np.exp2(rng.integers(-2, 3, shape[:-1] + (1,)))).astype(BF))
def wide(rng, *shape, cols=0):
    v = rng.standard_normal(shape, dtype=np.float32) * np.exp2(rng.integers(-12, 13, shape)).astype(np.float32)
    if cols: v *= np.repeat(np.exp2(rng.integers(-cols, cols + 1, shape[:-2] + (1, shape[-1] // 4))) * (rng.random(shape[:-2] + (1, shape[-1] // 4)) > 0.0625), 4, axis=-1).astype(np.float32)
    return mx_ref.flush(v.astype(BF))
K = 384
def plant(t, k, v):
    o = t.astype(np.float32).reshape(128, -1, 4); o[:, k] = v
    return o.reshape(128, -1).astype(BF)
def setup_inputs(rng):
    return {"x": f(rng, N, 128, 512), "c1": f(rng, N, 128, 4 * K), "c2": f(rng, N, 128, 4 * K)}
def setup_inputs_last(rng):
    d = setup_inputs(rng); u = f(rng, 128, 4).astype(np.float32).reshape(128, 1, 4); x = []
    s = np.exp2(np.where(np.arange(128) < 120, 2, 0) + np.arange(128) % 2).astype(np.float32).reshape(1, 128, 1)
    for r in range(N):
        x.append(plant(d["x"][r], rng.permutation(128), u * s))
    d["x"] = np.stack(x)
    for c in ("c1", "c2"):
        d[c] = np.stack([plant(d[c][q], [K - 1], np.float32(2) * u) if q == N - 1 else d[c][q] for q in range(N)])
    return d
def setup_inputs_negative(rng):
    d = setup_inputs(rng)
    for c, s in (("x", 1), ("c1", -1), ("c2", -1)):
        d[c] = (np.abs(d[c].astype(np.float32)) * np.float32(s * 2.0 ** 20)).astype(BF)
    return d
def setup_inputs_own(rng):
    d = setup_inputs(rng)
    for c, s in (("c1", 2), ("c2", -2)):
        d[c] = np.stack([plant(d[c][r], rng.permutation(K)[:128], np.float32(s) * d["x"][r].astype(np.float32).reshape(128, -1, 4)) for r in range(N)])
    return d
def setup_inputs_spread(rng):
    d = setup_inputs(rng); d["x"] = wide(rng, N, 128, 512, cols=8)
    for c in ("c1", "c2"): d[c] = wide(rng, N, 128, 4 * K, cols=2)
    return d
def setup_inputs_ties(rng):
    d = setup_inputs(rng)
    d["x"] = np.stack([plant(d["x"][r], rng.permutation(128)[:1], np.zeros((128, 1, 4), np.float32)) for r in range(N)])
    for c in ("c1", "c2"):
        a = f(rng, N, 128, K)
        d[c] = np.stack([cols(np.concatenate([a[q], a[q], a[(q + 1) % N], a[(q + 2) % N]], axis=1), rng.permutation(K)) for q in range(N)])
    return d
def check_inputs(d):
    b = []
    for c in ("x", "c1", "c2"):
        a = np.abs(d[c].astype(np.float32))
        if not (np.isfinite(a) & ((a == 0) | ((a >= 2.0 ** -30) & (a <= 2.0 ** 30)))).all(): b.append(c)
    return b
def winners(v, book):
    s = np.concatenate([mx_ref.matmul(v, q) for q in book], axis=1)
    w = np.argmax(s + np.float32(0), axis=1)
    return w, s[np.arange(128), w]
def chosen(t, e):
    return t.reshape(128, -1, 4)[:, e].reshape(128, -1)
def reference(x, c1, c2):
    q1 = [mx_ref.quantize(c1[q]) for q in range(N)]
    q2 = [mx_ref.quantize(c2[q]) for q in range(N)]
    d1 = np.concatenate([decode(q) for q in q1], axis=1)
    d2 = np.concatenate([decode(q) for q in q2], axis=1)
    y = np.zeros((N, 128, 512), np.float32); no = np.zeros((N, 4, 128), np.float32)
    for r in range(N):
        w1, s1 = winners(mx_ref.quantize(x[r]), q1)
        R = (x[r].astype(np.float32) - chosen(d1, w1)).astype(BF)
        w2, s2 = winners(mx_ref.quantize(R), q2)
        y[r] = R.astype(np.float32) - chosen(d2, w2)
        no[r, 0] = w1; no[r, 1] = w2; no[r, 2] = s1; no[r, 3] = s2
    return {"y": y, "no": no}

@@ -1,0 +1,396 @@
+from concourse.bass import DstId, RemoteDMATransfer
+from concourse.mybir import dt, AluOpType, AxisListType, ActivationFunctionType
+
+N, K = 8, 384
+W1 = K + 7 * 128
+W2 = 4 * K + 4 * 128
+BIG = 1000000.0
+LOW = -9.0e29
+
+F, B, C8, U8, I32, U16 = "float32", "bfloat16", "float8_e4m3fn_x4", "uint8", "int32", "uint16"
+
+
+def sb(n, d):
+    return ("sbuf", [128, n], d)
+
+
+SCRATCH = {
+    "xt": ("sbuf", [128, 64, 8], B), "xs": sb(512, B), "xv": sb(512, B), "c1t": sb(4 * K, B), "c2t": sb(4 * K, B),
+    "c1p": sb(4 * K, B), "c2p": sb(4 * K, B),
+    "ones": sb(128, B), "ident": sb(128, B), "et": sb(2048, B), "eqc": sb(512, C8), "eqs": sb(512, U8), "lim": sb(K, B),
+    "xqc": sb(1024, C8), "xqs": sb(1024, U8), "rqc": sb(1024, C8), "rqs": sb(1024, U8),
+    "q1c": sb(K, C8), "q1s": sb(K, U8), "q2c": sb(4 * K, C8), "q2s": sb(4 * K, U8),
+    "run": sb(16 * K, F), "junk": sb(16 * K, B),
+    "mia": sb(6, F), "mib": sb(8, F), "mic": sb(8, F), "cva": sb(48, F), "cvb": sb(64, F), "cvc": sb(64, F),
+    "ofa": sb(24, U16), "ofb": sb(32, U16), "ofc": sb(32, U16),
+    "gta": sb(1536, B), "gtb": sb(2048, B), "gtc": sb(2048, B),
+    "sac": sb(384, C8), "sas": sb(384, U8), "sbc": sb(512, C8), "sbs": sb(512, U8), "scc": sb(512, C8), "scs": sb(512, U8),
+    "kac": sb(384, C8), "kas": sb(384, U8), "kbc": sb(512, C8), "kbs": sb(512, U8), "kcc": sb(512, C8), "kcs": sb(512, U8),
+    "sci1": sb(32, F), "sci2": sb(32, F), "tab1": sb(4 * W1, F), "tab2": sb(4 * W2, F),
+    "pen1": sb(8, F), "pen2": sb(8, F), "tp1": sb(8, F), "tp2": sb(8, F), "tn1": sb(8, F), "tn2": sb(8, F),
+    "pp1": sb(8, F), "pp2": sb(8, F), "nb": sb(8, F), "num1": sb(8, F), "num2": sb(8, F),
+    "pos1": sb(1, F), "pos2": sb(1, F), "cvp1": sb(8, F), "cvp2": sb(8, F), "ofp1": sb(8, U16), "ofp2": sb(8, U16),
+    "wp1": sb(32, F), "wt1": sb(32, F), "il": sb(256, F), "ou": sb(256, F), "wp2": sb(2, F), "nc": sb(32, F), "nct": sb(32, F),
+    "pi": sb(1, I32), "ia": sb(1, I32), "ib": sb(1, I32), "iu": sb(1, I32), "it": sb(1, I32), "iw": sb(32, I32),
+    "fa": sb(1, F), "fu": sb(1, F), "jv": sb(1, F), "ut": sb(1, F), "lrn": sb(32, U16),
+    "rt": sb(512, B), "rn": sb(512, B), "yt": sb(512, F),
+}
+for _b in range(8):
+    SCRATCH["p%d" % _b] = ("psum", [128, 512], F)
+SEMAPHORES = (["pv", "ps", "pt", "pg", "ls", "lx", "lc1", "lc2", "cva", "cvb", "cvc", "cvp1", "cvp2", "il", "no1", "nc", "no2",
+               "yo", "ac2", "as1", "as2", "aka", "akb", "akc"]
+              + ["ax%d" % q for q in range(N)] + ["ar%d" % q for q in range(N)])
+
+
+def rank_program(g, core, T, topo):
+    me = T.rank_of(core)
+    if me is None:
+        return
+    A, X, FN = AluOpType, AxisListType.X, ActivationFunctionType
+    ranks = list(range(N))
+
+    def same(a, b):
+        return topo.die(T.cores[a]) == topo.die(T.cores[b])
+
+    def home_of(r):
+        return [q for q in ranks if same(q, r)]
+
+    def mates_of(r):
+        return [q for q in ranks if q != r and same(q, r)]
+
+    def far_of(r):
+        return [q for q in ranks if not same(q, r)]
+
+    home, mates, far = home_of(me), mates_of(me), far_of(me)
+    sem = T.sem
+    queue = {"v": g.vector, "s": g.scalar, "t": g.tensor, "g": g, "y": g.sync}
+    count, seen, local, total = {}, {}, [0], {}
+
+    def need(qn, deps):
+        top = {}
+        for s, v in deps:
+            top[s] = max(top.get(s, 0), v)
+        for s in sorted(top):
+            if seen.get((qn, s), 0) < top[s]:
+                queue[qn].wait_ge(sem[s], top[s])
+                seen[(qn, s)] = top[s]
+
+    def did(name, ins):
+        ins.then_inc(sem[name], 1)
+        count[name] = count.get(name, 0) + 1
+        return (name, count[name])
+
+    def V(deps, call, *a, **k):
+        need("v", deps)
+        return did("pv", call(*a, **k))
+
+    def S(deps, call, *a, **k):
+        need("s", deps)
+        return did("ps", call(*a, **k))
+
+    def G(deps, call, *a, **k):
+        need("g", deps)
+        return did("pg", call(*a, **k))
+
+    def D(qn, deps, name, out, in_):
+        need(qn, deps)
+        queue[qn].dma_start(out, in_).then_inc(sem[name], 16)
+        total[name] = total.get(name, 0) + 16
+        return (name, total[name])
+
+    vec, act = g.vector, g.scalar.activation
+
+    def send(deps, name, items):
+        need("g", deps)
+        n = 1
+        while n < len(items):
+            n *= 2
+        tr = []
+        for k, (dst, s, d) in enumerate(items):
+            eng = topo.engines(core, T.cores[dst[0]])
+            per = len(eng) // n
+            mask = 0
+            for e in eng[k * per:(k + 1) * per]:
+                mask |= 1 << e
+            ids = []
+            for q in dst:
+                rid, pid, _ = topo.addr(T.cores[q])
+                ids.append(DstId(rid=rid, pnc=pid))
+            tr.append(RemoteDMATransfer(dst_ids=ids, dma_engine_mask=mask, remote_sem=sem[name], srcs=[s], dsts=[d] * len(ids)))
+            local[0] += per
+        g.remote_dma_fused(tr, local_sem=sem.ls)
+
+    def width(n):
+        eng = len(topo.engines(core, T.cores[(me + 1) % N]))
+        k = 1
+        while k < n:
+            k *= 2
+        return eng // k
+
+    def u8(t, a, b):
+        return t[:, a:b].bitcast(dt.uint8)
+
+    bank = [T["p%d" % b] for b in range(8)]
+    free = [[] for _ in range(8)]
+
+    def mm(b, n, lc, lsc, la, rc, rsc, ra, deps):
+        need("t", deps + free[b])
+        return did("pt", g.tensor.matmul_mx(bank[b][:, 0:n], lc[:, la:la + 128], lsc[:, la:la + 128],
+                                            rc[:, ra:ra + n], rsc[:, ra:ra + n], True, True))
+
+    def evac(qn, b, n, tab, w, t, runs, dep):
+        tk = []
+        for src, dst, m in runs:
+            o, i = tab[:, t * w + dst:t * w + dst + m], bank[b][:, src:src + m]
+            if qn == "v":
+                tk.append(V([dep], vec.tensor_scalar, o, i, -1.0, None, A.mult))
+            else:
+                tk.append(S([dep], act, o, i, FN.Copy, scale=-1.0))
+        free[b] = tk
+        return tk
+
+    base1, base2, a1, a2 = [], [], 0, 0
+    for q in ranks:
+        base1.append(a1)
+        base2.append(a2)
+        a1 += K if q == me else 128
+        a2 += K if q in home else 128
+
+    def runs_of(group, base):
+        out = []
+        for k, q in enumerate(group):
+            if out and out[-1][1] + out[-1][2] == base[q]:
+                out[-1] = (out[-1][0], out[-1][1], out[-1][2] + 128)
+            else:
+                out.append((128 * k, base[q], 128))
+        return out
+
+    dx = D("y", [], "lx", T.xt[:, :, :], T.x[:, :])
+    d1 = D("s", [], "lc1", T.c1t[:, :], T.c1[:, :])
+    d2 = D("y", [], "lc2", T.c2t[:, :], T.c2[:, :])
+
+    o1 = V([], vec.memset, T.ones[:, :], 1.0)
+    i1 = G([o1], g.affine_select, T.ident[:, :], T.ones[:, :], [[-1, 128]], A.is_equal, 0.0, 0, 1)
+    i2 = G([], g.iota, T.pi[:, :], [[0, 1]], 0, 1)
+    i3 = G([], g.iota, T.iw[:, :], [[4, 8], [128, 4]], 0, 0)
+    i4 = G([], g.iota, T.nb[:, :], [[K, 8]], 0, 0, allow_small_or_imprecise_dtypes=True)
+    ez = V([], vec.memset, T.et[:, :], 0.0)
+    lm = V([], vec.memset, T.lim[:, :], LOW)
+
+    u0 = V([dx], vec.tensor_copy, T.xs[:, 0:256], T.xt[:, :, 0:4])
+    u1 = S([dx], act, T.xs[:, 256:512], T.xt[:, :, 4:8], FN.Copy)
+    m0 = 128 * me
+    qx = V([u0, u1], vec.quantize_mx, T.xqc[:, m0:m0 + 128], T.xqs[:, m0:m0 + 128], T.xs[:, :])
+    others = mates + far
+    send([qx], "ax%d" % me, [(others, u8(T.xqc, m0, m0 + 128), u8(T.xqc, m0, m0 + 128))])
+    send([qx], "ax%d" % me, [(others, T.xqs[:, m0:m0 + 128], T.xqs[:, m0:m0 + 128])])
+
+    ec = [V([i1, ez], vec.tensor_copy, T.et[:, 512 * b + b:512 * (b + 1):4], T.ident[:, :]) for b in range(4)]
+    qe = V(ec, vec.quantize_mx, T.eqc[:, :], T.eqs[:, :], T.et[:, :])
+    q1 = V([d1], vec.quantize_mx, T.q1c[:, :], T.q1s[:, :], T.c1t[:, :])
+    pl1 = [V([d1], vec.tensor_copy, T.c1p[:, K * t:K * (t + 1)], T.c1t[:, t:4 * K:4]) for t in (0, 1)]
+
+    ka = V([i2], vec.tensor_scalar, T.ia[:, :], T.pi[:, :], 7, None, A.bitwise_and)
+    kb = V([i2], vec.tensor_scalar, T.ib[:, :], T.pi[:, :], 3, None, A.arith_shift_right)
+    ku = V([i2], vec.tensor_scalar, T.iu[:, :], T.pi[:, :], 2, 3, A.arith_shift_right, A.bitwise_and)
+    kt = V([i2], vec.tensor_scalar, T.it[:, :], T.pi[:, :], 3, None, A.bitwise_and)
+    kf = V([ka], vec.tensor_scalar, T.fa[:, :], T.ia[:, :], 16.0, None, A.mult)
+    kg = V([ku], vec.tensor_scalar, T.fu[:, :], T.iu[:, :], 32.0, None, A.mult)
+    jv = V([kf, kb], vec.tensor_tensor, T.jv[:, :], T.fa[:, :], T.ib[:, :], A.add)
+    kh = V([kg, kt], vec.tensor_tensor, T.ut[:, :], T.fu[:, :], T.it[:, :], A.add)
+    lr = V([kh, i3], vec.tensor_scalar, T.lrn[:, :], T.iw[:, :], T.ut[:, :], None, A.add)
+
+    pl1 += [S([d1], act, T.c1p[:, K * t:K * (t + 1)], T.c1t[:, t:4 * K:4], FN.Copy) for t in (2, 3)]
+
+    score_no = [0]
+
+    def scan(b, dep):
+        k = score_no[0]
+        score_no[0] += 1
+        tk = V([dep, lm], vec.tensor_tensor_scan, T.run[:, K * k:K * (k + 1)], bank[b][:, 0:K], T.lim[:, :], LOW, A.max, A.max)
+        free[b] = [tk]
+        return k, tk
+
+    def sign(k, tk, acc):
+        return S([tk], act, T.junk[:, K * k:K * (k + 1)], T.run[:, K * k:K * (k + 1)], FN.Sign,
+                 bias=T.run[:, K * (k + 1) - 1:K * (k + 1)], scale=-1.0, accum_out=acc)
+
+    so = mm(4, K, T.xqc, T.xqs, m0, T.q1c, T.q1s, 0, [qx, q1])
+    to = [mm(b, K, T.eqc, T.eqs, 128 * b, T.q1c, T.q1s, 0, [qe, q1]) for b in range(4)]
+    k0, s0 = scan(4, so)
+    n0 = sign(k0, s0, T.sci1[:, 4 * me + 1:4 * me + 2])
+    ow = [V([s0], vec.tensor_copy, T.sci1[:, 4 * me:4 * me + 1], T.run[:, K * (k0 + 1) - 1:K * (k0 + 1)])]
+    t1 = [[], [], [], []]
+    for b in range(4):
+        t1[b] += evac("v" if b < 2 else "s", b, K, T.tab1, W1, b, [(0, base1[me], K)], to[b])
+    hm = K * home.index(me)
+    q2 = V([d2], vec.quantize_mx, T.q2c[:, hm:hm + K], T.q2s[:, hm:hm + K], T.c2t[:, :])
+    send([q2], "ac2", [(mates, u8(T.q2c, hm, hm + K), u8(T.q2c, hm, hm + K))])
+    send([q2], "ac2", [(mates, T.q2s[:, hm:hm + K], T.q2s[:, hm:hm + K])])
+    wz = V([], vec.memset, T.wp1[:, :], 0.0)
+    nz = V([], vec.memset, T.nc[:, :], 0.0)
+    p1 = []
+    for q in others:
+        p1.append(V([jv], vec.tensor_scalar, T.pp1[:, q:q + 1], T.jv[:, :], float(base1[q]), None, A.add))
+    xv = S([u0, u1, lr], act, T.xv[:, :], T.xs[:, 0:512].indirect(T.lrn[:, 0:32]), FN.Copy)
+
+    def score(group, banks, rc, rs, qc, qs, arrived, dw):
+        return [mm(banks[i], K, rc, rs, 128 * q, qc, qs, dw, [arrived(q)]) for i, q in enumerate(group)]
+
+    def search(group, banks, tks, mi):
+        n = len(group)
+        sc = [scan(banks[i], tks[i]) for i in range(n)]
+        first = sc[0][0]
+        mx = V([s for _, s in sc], vec.tensor_copy, mi[:, 0:2 * n:2], T.run[:, K * (first + 1) - 1:K * (first + n):K])
+        sg = [sign(k, tk, mi[:, 2 * i + 1:2 * i + 2]) for i, (k, tk) in enumerate(sc)]
+        return [mx] + sg
+
+    def spread(name, src, dst, deps, queues):
+        for k in range(8):
+            D(queues[k % len(queues)], deps, name, dst[16 * k:16 * (k + 1), :], src[:, :])
+        return (name, total[name])
+
+    def relist(n, cv, of, dep):
+        return [V([dep], vec.tensor_copy, of[:, 8 * k:8 * (k + 1)], cv[:, 2 * k + 1:16 * n:2 * n]) for k in range(n)]
+
+    def gather(n, of, win, gt, deps):
+        tk = []
+        for t in (0, 1):
+            tk.append(V(deps, vec.tensor_copy, gt[:, t:512 * n:4], win[:, K * t:K * (t + 1)].indirect(of[:, 0:8 * n])))
+        for t in (2, 3):
+            tk.append(S(deps, act, gt[:, t:512 * n:4], win[:, K * t:K * (t + 1)].indirect(of[:, 0:8 * n]), FN.Copy))
+        return tk
+
+    def give(group, cc, cs, dep, name, kc, ks, slot):
+        send([dep], name, [([q], u8(cc, 128 * i, 128 * (i + 1)), u8(kc, 128 * slot(q), 128 * (slot(q) + 1)))
+                           for i, q in enumerate(group)])
+        send([dep], name, [([q], cs[:, 128 * i:128 * (i + 1)], ks[:, 128 * slot(q):128 * (slot(q) + 1)])
+                           for i, q in enumerate(group)])
+
+    def tell(group, mi, deps, name, sci):
+        send(deps, name, [([q], mi[:, 2 * i:2 * i + 2], sci[:, 4 * me:4 * me + 2]) for i, q in enumerate(group)])
+
+    def slot_a(q):
+        return mates_of(q).index(me)
+
+    def slot_b(q):
+        return far_of(q).index(me)
+
+    wx = 2 * width(1)
+    ma = score(mates, [5, 6, 7], T.xqc, T.xqs, T.q1c, T.q1s, lambda q: ("ax%d" % q, wx), 0)
+    mb = score(far, [0, 1, 2, 3], T.xqc, T.xqs, T.q1c, T.q1s, lambda q: ("ax%d" % q, wx), 0)
+    sa = search(mates, [5, 6, 7], ma, T.mia)
+    ca = spread("cva", T.mia, T.cva, sa, ["y"])
+    tell(mates, T.mia, sa, "as1", T.sci1)
+    sbt = search(far, [0, 1, 2, 3], mb, T.mib)
+    cb = spread("cvb", T.mib, T.cvb, sbt, ["y", "s"])
+    tell(far, T.mib, sbt, "as1", T.sci1)
+    la = relist(3, T.cva, T.ofa, ca)
+    ga = gather(3, T.ofa, T.c1p, T.gta, la + pl1)
+    qa = V(ga, vec.quantize_mx, T.sac[:, :], T.sas[:, :], T.gta[:, :])
+    give(mates, T.sac, T.sas, qa, "aka", T.kac, T.kas, slot_a)
+    lb = relist(4, T.cvb, T.ofb, cb)
+    gb = gather(4, T.ofb, T.c1p, T.gtb, lb + pl1)
+    qb = V(gb, vec.quantize_mx, T.sbc[:, :], T.sbs[:, :], T.gtb[:, :])
+    give(far, T.sbc, T.sbs, qb, "akb", T.kbc, T.kbs, slot_b)
+
+    def choose(sci, pen, tp, pp, pos, mxo, deps):
+        sc = sci[:, 0:32:4]
+        a = V(deps, vec.tensor_reduce, mxo, sc, X, A.max)
+        b = V([a], vec.tensor_scalar, pen[:, :], sc, mxo, BIG, A.is_lt, A.mult)
+        c = V([b], vec.tensor_tensor, tp[:, :], pen[:, :], pp[:, :], A.add)
+        return a, b, V([c], vec.tensor_reduce, pos[:, :], tp[:, :], X, A.min)
+
+    def number(sci, num, pen, tn, wo, deps):
+        a = V(deps, vec.tensor_tensor, num[:, :], sci[:, 1:32:4], T.nb[:, :], A.add)
+        b = V([a], vec.tensor_tensor, tn[:, :], pen[:, :], num[:, :], A.add)
+        return V([b], vec.tensor_reduce, wo, tn[:, :], X, A.min)
+
+    po = V([n0, jv], vec.tensor_scalar, T.pp1[:, me:me + 1], T.sci1[:, 4 * me + 1:4 * me + 2], float(base1[me]), None, A.add)
+    w4 = width(3)
+    ars1 = ("as1", 3 * width(3) + 4 * width(4))
+    c1a, c1b, c1c = choose(T.sci1, T.pen1, T.tp1, T.pp1, T.pos1, T.wp1[:, 1:2], [ars1, po, n0, wz] + p1 + ow)
+    cp1 = spread("cvp1", T.pos1, T.cvp1, [c1c], ["y"])
+
+    to2 = [mm(4 + b, K, T.eqc, T.eqs, 128 * b, T.q2c, T.q2s, hm, [q2, qe]) for b in range(4)]
+    t2 = [[], [], [], []]
+
+    def mate_table(b0, q, tks):
+        for b in range(4):
+            t2[b] += evac("v" if b < 2 else "s", b0 + b, K, T.tab2, W2, b, [(0, base2[q], K)], tks[b])
+
+    mate_table(4, me, to2)
+    da = [mm(b, 384, T.eqc, T.eqs, 128 * b, T.kac, T.kas, 0, [("aka", 2 * 3 * width(3)), qe]) for b in range(4)]
+    pl2 = [V([d2], vec.tensor_copy, T.c2p[:, K * t:K * (t + 1)], T.c2t[:, t:4 * K:4]) for t in (0, 1)]
+    pl2 += [S([d2], act, T.c2p[:, K * t:K * (t + 1)], T.c2t[:, t:4 * K:4], FN.Copy) for t in (2, 3)]
+    ra = runs_of(mates, base1)
+    for b in range(4):
+        t1[b] += evac("v" if b < 2 else "s", b, 384, T.tab1, W1, b, ra, da[b])
+    nu1 = number(T.sci1, T.num1, T.pen1, T.tn1, T.wp1[:, 0:1], [ars1, n0, i4, c1b, wz])
+    wt = V([nu1, c1a], vec.transpose, T.wt1[:, :], T.wp1[:, :])
+    of1 = V([cp1], vec.tensor_copy, T.ofp1[:, :], T.cvp1[:, :])
+
+    db = [mm(4 + b, 512, T.eqc, T.eqs, 128 * b, T.kbc, T.kbs, 0, [("akb", 2 * 4 * width(4)), qe]) for b in range(4)]
+    rb = runs_of(far, base1)
+    for b in range(4):
+        t1[b] += evac("v" if b < 1 else "s", 4 + b, 512, T.tab1, W1, b, rb, db[b])
+    rr = [V([of1, xv] + t1[t], vec.tensor_tensor, T.rt[:, t:512:4], T.tab1[:, W1 * t:W1 * (t + 1)].indirect(T.ofp1[:, 0:8]),
+            T.xv[:, t:512:4], A.add) for t in range(4)]
+    qr = V(rr, vec.quantize_mx, T.rqc[:, m0:m0 + 128], T.rqs[:, m0:m0 + 128], T.rt[:, :])
+    send([qr], "ar%d" % me, [(far, u8(T.rqc, m0, m0 + 128), u8(T.rqc, m0, m0 + 128))])
+    send([qr], "ar%d" % me, [(far, T.rqs[:, m0:m0 + 128], T.rqs[:, m0:m0 + 128])])
+
+    ac2 = ("ac2", 3 * 2 * width(1))
+    ml = [mm(i, K, T.rqc, T.rqs, m0, T.q2c, T.q2s, K * i, [qr, q2, ac2]) for i in range(4)]
+    m1 = [mm(4 + b, K, T.eqc, T.eqs, 128 * b, T.q2c, T.q2s, K * home.index(mates[0]), [ac2, qe]) for b in range(4)]
+    sl = [scan(i, ml[i]) for i in range(4)]
+    lo = []
+    for (k, tk), q in zip(sl, home):
+        lo.append(sign(k, tk, T.sci2[:, 4 * q + 1:4 * q + 2]))
+    for (k, tk), q in zip(sl, home):
+        lo.append(V([tk], vec.tensor_copy, T.sci2[:, 4 * q:4 * q + 1], T.run[:, K * (k + 1) - 1:K * (k + 1)]))
+    rn = S(rr + [lr], act, T.rn[:, :], T.rt[:, 0:512].indirect(T.lrn[:, 0:32]), FN.Copy)
+    mate_table(4, mates[0], m1)
+    il = [D("y", [wt], "il", T.il[0:1, 128 * c:128 * (c + 1)], T.wt1[c:128:32, 0:32]) for c in range(2)]
+    mc = score(far, [0, 1, 2, 3], T.rqc, T.rqs, T.q2c, T.q2s, lambda q: ("ar%d" % q, wx), hm)
+    sct = search(far, [0, 1, 2, 3], mc, T.mic)
+    cc = spread("cvc", T.mic, T.cvc, sct, ["y", "s"])
+    tell(far, T.mic, sct, "as2", T.sci2)
+    m2 = [mm(4 + b, K, T.eqc, T.eqs, 128 * b, T.q2c, T.q2s, K * home.index(mates[1]), [ac2, qe]) for b in range(4)]
+    mate_table(4, mates[1], m2)
+    lc = relist(4, T.cvc, T.ofc, cc)
+    gc = gather(4, T.ofc, T.c2p, T.gtc, lc + pl2)
+    qc = V(gc, vec.quantize_mx, T.scc[:, :], T.scs[:, :], T.gtc[:, :])
+    give(far, T.scc, T.scs, qc, "akc", T.kcc, T.kcs, slot_b)
+
+    p2 = []
+    for q in ranks:
+        if q in home:
+            p2.append(V(lo, vec.tensor_scalar, T.pp2[:, q:q + 1], T.sci2[:, 4 * q + 1:4 * q + 2], float(base2[q]), None, A.add))
+        else:
+            p2.append(V([jv], vec.tensor_scalar, T.pp2[:, q:q + 1], T.jv[:, :], float(base2[q]), None, A.add))
+    ars2 = ("as2", 4 * width(4))
+    c2a, c2b, c2c = choose(T.sci2, T.pen2, T.tp2, T.pp2, T.pos2, T.wp2[:, 1:2], [ars2] + p2 + lo)
+    cp2 = spread("cvp2", T.pos2, T.cvp2, [c2c], ["y"])
+    nu2 = number(T.sci2, T.num2, T.pen2, T.tn2, T.wp2[:, 0:1], [ars2, i4, c2b] + lo)
+    m3 = [mm(b, K, T.eqc, T.eqs, 128 * b, T.q2c, T.q2s, K * home.index(mates[2]), [ac2, qe]) for b in range(4)]
+    mate_table(0, mates[2], m3)
+    dn = D("y", [nu2, c2a, nz], "nc", T.nc[0:16, 0:16], T.wp2[:, :])
+    ov = [V([il[1]], vec.tensor_copy, T.ou[0:1, 128 * c + h:128 * (c + 1):2], T.il[0:1, 128 * c + 64 * h:128 * c + 64 * (h + 1)])
+          for c in range(2) for h in range(2)]
+    D("y", ov, "no1", T.no[0:3:2, :], T.ou[0:1, :])
+    of2 = V([cp2], vec.tensor_copy, T.ofp2[:, :], T.cvp2[:, :])
+    nt = V([dn], vec.transpose, T.nct[0:32, :], T.nc[0:32, :])
+    D("y", [nt], "no2", T.no[1, :], T.nct[0:16:2, 0:16])
+    D("y", [nt], "no2", T.no[3, :], T.nct[1:16:2, 0:16])
+
+    dc = [mm(4 + b, 512, T.eqc, T.eqs, 128 * b, T.kcc, T.kcs, 0, [("akc", 2 * 4 * width(4)), qe]) for b in range(4)]
+    rc = runs_of(far, base2)
+    for b in range(4):
+        t2[b] += evac("v" if b < 1 else "s", 4 + b, 512, T.tab2, W2, b, rc, dc[b])
+    yy = [V([of2, rn] + t2[t], vec.tensor_tensor, T.yt[:, t:512:4], T.tab2[:, W2 * t:W2 * (t + 1)].indirect(T.ofp2[:, 0:8]),
+            T.rn[:, t:512:4], A.add) for t in range(4)]
+    D("y", yy, "yo", T.y[:, :], T.yt[:, :])
+
+    need("g", [(n, count[n]) for n in count] + [("ls", local[0])])
+    need("y", [(n, total[n]) for n in total])

@@ -7,6 +7,15 @@ W2 = 4 * K + 4 * 128
 BIG = 1000000.0
 LOW = -9.0e29
 
+OUT1, OUT2 = [3, 4], [4]
+BACK1, BACK2 = [4, 3], [2, 2]
+STEPS1 = ["00v", "02s", "01v", "03s", "0", "11s", "10v", "12s", "13s", "1"]
+STEPS2 = ["00v", "02s", "01v", "03s", "0", "11s", "12s", "10v", "13v", "1"]
+EVAC1, EVAC2 = ["vvss", "vsvs"], ["vsss", "vsvs"]
+HELD = {"early": ["00v", "01s", "02s", "03s"], "list1": [], "wait2": ["10s", "11s", "12s", "13s", "20s", "21s"], "wait3": [], "list2": ["30s", "31s"], "wait4": ["32s", "33s", "22s", "23s"]}
+PLANES = {"early": [], "lent": ["10g", "11g", "12g", "13g"], "wait2": ["20g", "21g"], "wait3": ["22g", "23g"]}
+STORE = [4, 4]
+
 F, B, C8, U8, I32, U16 = "float32", "bfloat16", "float8_e4m3fn_x4", "uint8", "int32", "uint16"
 
 
@@ -15,31 +24,25 @@ def sb(n, d):
 
 
 SCRATCH = {
-    "xt": ("sbuf", [128, 64, 8], B), "xs": sb(512, B), "xv": sb(512, B), "c1t": sb(4 * K, B), "c2t": sb(4 * K, B),
-    "c1p": sb(4 * K, B), "c2p": sb(4 * K, B),
+    "xt": sb(512, B), "c1t": sb(4 * K, B), "c2t": sb(4 * K, B), "c1p": sb(4 * K, B), "c2p": sb(4 * K, B),
     "ones": sb(128, B), "ident": sb(128, B), "et": sb(2048, B), "eqc": sb(512, C8), "eqs": sb(512, U8), "lim": sb(K, B),
     "xqc": sb(1024, C8), "xqs": sb(1024, U8), "rqc": sb(1024, C8), "rqs": sb(1024, U8),
     "q1c": sb(K, C8), "q1s": sb(K, U8), "q2c": sb(4 * K, C8), "q2s": sb(4 * K, U8),
     "run": sb(16 * K, F), "junk": sb(16 * K, B),
-    "mia": sb(6, F), "mib": sb(8, F), "mic": sb(8, F), "cva": sb(48, F), "cvb": sb(64, F), "cvc": sb(64, F),
-    "ofa": sb(24, U16), "ofb": sb(32, U16), "ofc": sb(32, U16),
-    "gta": sb(1536, B), "gtb": sb(2048, B), "gtc": sb(2048, B),
-    "sac": sb(384, C8), "sas": sb(384, U8), "sbc": sb(512, C8), "sbs": sb(512, U8), "scc": sb(512, C8), "scs": sb(512, U8),
-    "kac": sb(384, C8), "kas": sb(384, U8), "kbc": sb(512, C8), "kbs": sb(512, U8), "kcc": sb(512, C8), "kcs": sb(512, U8),
-    "sci1": sb(32, F), "sci2": sb(32, F), "tab1": sb(4 * W1, F), "tab2": sb(4 * W2, F),
-    "pen1": sb(8, F), "pen2": sb(8, F), "tp1": sb(8, F), "tp2": sb(8, F), "tn1": sb(8, F), "tn2": sb(8, F),
-    "pp1": sb(8, F), "pp2": sb(8, F), "nb": sb(8, F), "num1": sb(8, F), "num2": sb(8, F),
-    "pos1": sb(1, F), "pos2": sb(1, F), "cvp1": sb(8, F), "cvp2": sb(8, F), "ofp1": sb(8, U16), "ofp2": sb(8, U16),
-    "wp1": sb(32, F), "wt1": sb(32, F), "il": sb(256, F), "ou": sb(256, F), "wp2": sb(2, F), "nc": sb(32, F), "nct": sb(32, F),
-    "pi": sb(1, I32), "ia": sb(1, I32), "ib": sb(1, I32), "iu": sb(1, I32), "it": sb(1, I32), "iw": sb(32, I32),
-    "fa": sb(1, F), "fu": sb(1, F), "jv": sb(1, F), "ut": sb(1, F), "lrn": sb(32, U16),
-    "rt": sb(512, B), "rn": sb(512, B), "yt": sb(512, F),
+    "gl": sb(128, F), "wl": ("sbuf", [128, 16, 16], F), "ol": sb(256, F),
+    "mi1": sb(16, F), "mi2": sb(8, F), "of1": sb(56, U16), "of2": sb(32, U16), "op1": sb(8, U16), "op2": sb(8, U16),
+    "gt1": sb(7 * 512, B), "gt2": sb(4 * 512, B),
+    "s1c": sb(896, C8), "s1s": sb(896, U8), "s2c": sb(512, C8), "s2s": sb(512, U8),
+    "k1c": sb(896, C8), "k1s": sb(896, U8), "k2c": sb(512, C8), "k2s": sb(512, U8),
+    "sci1": sb(32, F), "sci2": sb(24, F), "tab1": sb(4 * W1, F), "tab2": sb(4 * W2, F),
+    "pp1": sb(8, F), "pp2": sb(6, F), "ix": sb(2, F), "ch1": sb(32, F), "ch2": sb(32, F),
+    "rt": sb(512, B), "yt": sb(512, F),
 }
 for _b in range(8):
     SCRATCH["p%d" % _b] = ("psum", [128, 512], F)
-SEMAPHORES = (["pv", "ps", "pt", "pg", "ls", "lx", "lc1", "lc2", "cva", "cvb", "cvc", "cvp1", "cvp2", "il", "no1", "nc", "no2",
-               "yo", "ac2", "as1", "as2", "aka", "akb", "akc"]
-              + ["ax%d" % q for q in range(N)] + ["ar%d" % q for q in range(N)])
+SEMAPHORES = (["pv", "ps", "pt", "pg", "ls", "lx", "lc1", "lc2", "no", "yo", "ac", "as1", "as2"]
+              + ["ax%d" % q for q in range(N)] + ["ar%d" % q for q in range(N)]
+              + ["k1%d" % b for b in range(len(BACK1))] + ["k2%d" % b for b in range(len(BACK2))])
 
 
 def rank_program(g, core, T, topo):
@@ -49,19 +52,16 @@ def rank_program(g, core, T, topo):
     A, X, FN = AluOpType, AxisListType.X, ActivationFunctionType
     ranks = list(range(N))
 
-    def same(a, b):
-        return topo.die(T.cores[a]) == topo.die(T.cores[b])
+    home = [q for q in ranks if topo.die(T.cores[q]) == topo.die(core)]
+    far = [q for q in ranks if q not in home]
+    place = home.index(me)
 
-    def home_of(r):
-        return [q for q in ranks if same(q, r)]
+    def turn(group, k):
+        return group[(place + k) % len(group)]
 
-    def mates_of(r):
-        return [q for q in ranks if q != r and same(q, r)]
-
-    def far_of(r):
-        return [q for q in ranks if not same(q, r)]
-
-    home, mates, far = home_of(me), mates_of(me), far_of(me)
+    out2, in2 = [turn(far, k) for k in range(4)], [turn(far, -k) for k in range(4)]
+    near_out, near_in = [turn(home, k) for k in (1, 2, 3)], [turn(home, -k) for k in (1, 2, 3)]
+    out1, in1 = out2 + near_out, in2 + near_in
     sem = T.sem
     queue = {"v": g.vector, "s": g.scalar, "t": g.tensor, "g": g, "y": g.sync}
     count, seen, local, total = {}, {}, [0], {}
@@ -99,18 +99,22 @@ def rank_program(g, core, T, topo):
         return (name, total[name])
 
     vec, act = g.vector, g.scalar.activation
+    engines = topo.engines(core, T.cores[(me + 1) % N])
+
+    def width(n):
+        k = 1
+        while k < n:
+            k *= 2
+        return len(engines) // k
 
     def send(deps, name, items):
         need("g", deps)
-        n = 1
-        while n < len(items):
-            n *= 2
+        per = width(len(items))
+        step = len(engines) // per
         tr = []
         for k, (dst, s, d) in enumerate(items):
-            eng = topo.engines(core, T.cores[dst[0]])
-            per = len(eng) // n
             mask = 0
-            for e in eng[k * per:(k + 1) * per]:
+            for e in engines[k::step]:
                 mask |= 1 << e
             ids = []
             for q in dst:
@@ -120,277 +124,210 @@ def rank_program(g, core, T, topo):
             local[0] += per
         g.remote_dma_fused(tr, local_sem=sem.ls)
 
-    def width(n):
-        eng = len(topo.engines(core, T.cores[(me + 1) % N]))
-        k = 1
-        while k < n:
-            k *= 2
-        return eng // k
-
     def u8(t, a, b):
         return t[:, a:b].bitcast(dt.uint8)
 
+    def cuts(sizes):
+        return [(sum(sizes[:b]), n) for b, n in enumerate(sizes)]
+
+    def spread(dep, name, qc, qs, a, b, dst, sizes):
+        for i, n in cuts(sizes):
+            send([dep], name, [(dst[i:i + n], qs[:, a:b], qs[:, a:b])])
+            send([dep], name, [(dst[i:i + n], u8(qc, a, b), u8(qc, a, b))])
+
     bank = [T["p%d" % b] for b in range(8)]
     free = [[] for _ in range(8)]
+    EVEN, ODD = [4, 0, 1, 2], [3, 5, 6, 7]
 
     def mm(b, n, lc, lsc, la, rc, rsc, ra, deps):
         need("t", deps + free[b])
         return did("pt", g.tensor.matmul_mx(bank[b][:, 0:n], lc[:, la:la + 128], lsc[:, la:la + 128],
                                             rc[:, ra:ra + n], rsc[:, ra:ra + n], True, True))
 
-    def evac(qn, b, n, tab, w, t, runs, dep):
-        tk = []
-        for src, dst, m in runs:
-            o, i = tab[:, t * w + dst:t * w + dst + m], bank[b][:, src:src + m]
-            if qn == "v":
-                tk.append(V([dep], vec.tensor_scalar, o, i, -1.0, None, A.mult))
-            else:
-                tk.append(S([dep], act, o, i, FN.Copy, scale=-1.0))
-        free[b] = tk
+    def unpack(b, t, n, qc, qs, a, dep):
+        return mm(b, n, T.eqc, T.eqs, 128 * t, qc, qs, a, [dep, qe])
+
+    def evac(qn, b, n, tab, a, dep):
+        o, i = tab[:, a:a + n], bank[b][:, 0:n]
+        if qn == "v":
+            tk = V([dep], vec.tensor_scalar, o, i, -1.0, None, A.mult)
+        else:
+            tk = S([dep], act, o, i, FN.Copy, scale=-1.0)
+        free[b] = [tk]
         return tk
 
-    base1, base2, a1, a2 = [], [], 0, 0
-    for q in ranks:
-        base1.append(a1)
-        base2.append(a2)
-        a1 += K if q == me else 128
-        a2 += K if q in home else 128
-
-    def runs_of(group, base):
-        out = []
-        for k, q in enumerate(group):
-            if out and out[-1][1] + out[-1][2] == base[q]:
-                out[-1] = (out[-1][0], out[-1][1], out[-1][2] + 128)
-            else:
-                out.append((128 * k, base[q], 128))
-        return out
-
-    dx = D("y", [], "lx", T.xt[:, :, :], T.x[:, :])
-    d1 = D("s", [], "lc1", T.c1t[:, :], T.c1[:, :])
+    dx = D("y", [], "lx", T.xt[:, :], T.x[:, :])
+    d1 = D("y", [], "lc1", T.c1t[:, :], T.c1[:, :])
     d2 = D("y", [], "lc2", T.c2t[:, :], T.c2[:, :])
 
     o1 = V([], vec.memset, T.ones[:, :], 1.0)
     i1 = G([o1], g.affine_select, T.ident[:, :], T.ones[:, :], [[-1, 128]], A.is_equal, 0.0, 0, 1)
-    i2 = G([], g.iota, T.pi[:, :], [[0, 1]], 0, 1)
-    i3 = G([], g.iota, T.iw[:, :], [[4, 8], [128, 4]], 0, 0)
-    i4 = G([], g.iota, T.nb[:, :], [[K, 8]], 0, 0, allow_small_or_imprecise_dtypes=True)
+    p1 = G([], g.iota, T.pp1[:, 0:7], [[128, 7]], K, 1, allow_small_or_imprecise_dtypes=True)
+    p2 = G([], g.iota, T.pp2[:, 0:4], [[128, 4]], 4 * K, 1, allow_small_or_imprecise_dtypes=True)
     ez = V([], vec.memset, T.et[:, :], 0.0)
-    lm = V([], vec.memset, T.lim[:, :], LOW)
-
-    u0 = V([dx], vec.tensor_copy, T.xs[:, 0:256], T.xt[:, :, 0:4])
-    u1 = S([dx], act, T.xs[:, 256:512], T.xt[:, :, 4:8], FN.Copy)
-    m0 = 128 * me
-    qx = V([u0, u1], vec.quantize_mx, T.xqc[:, m0:m0 + 128], T.xqs[:, m0:m0 + 128], T.xs[:, :])
-    others = mates + far
-    send([qx], "ax%d" % me, [(others, u8(T.xqc, m0, m0 + 128), u8(T.xqc, m0, m0 + 128))])
-    send([qx], "ax%d" % me, [(others, T.xqs[:, m0:m0 + 128], T.xqs[:, m0:m0 + 128])])
-
     ec = [V([i1, ez], vec.tensor_copy, T.et[:, 512 * b + b:512 * (b + 1):4], T.ident[:, :]) for b in range(4)]
+
+    m0 = 128 * me
+    qx = V([dx], vec.quantize_mx, T.xqc[:, m0:m0 + 128], T.xqs[:, m0:m0 + 128], T.xt[:, :])
+    spread(qx, "ax%d" % me, T.xqc, T.xqs, m0, m0 + 128, out1, OUT1)
     qe = V(ec, vec.quantize_mx, T.eqc[:, :], T.eqs[:, :], T.et[:, :])
-    q1 = V([d1], vec.quantize_mx, T.q1c[:, :], T.q1s[:, :], T.c1t[:, :])
-    pl1 = [V([d1], vec.tensor_copy, T.c1p[:, K * t:K * (t + 1)], T.c1t[:, t:4 * K:4]) for t in (0, 1)]
-
-    ka = V([i2], vec.tensor_scalar, T.ia[:, :], T.pi[:, :], 7, None, A.bitwise_and)
-    kb = V([i2], vec.tensor_scalar, T.ib[:, :], T.pi[:, :], 3, None, A.arith_shift_right)
-    ku = V([i2], vec.tensor_scalar, T.iu[:, :], T.pi[:, :], 2, 3, A.arith_shift_right, A.bitwise_and)
-    kt = V([i2], vec.tensor_scalar, T.it[:, :], T.pi[:, :], 3, None, A.bitwise_and)
-    kf = V([ka], vec.tensor_scalar, T.fa[:, :], T.ia[:, :], 16.0, None, A.mult)
-    kg = V([ku], vec.tensor_scalar, T.fu[:, :], T.iu[:, :], 32.0, None, A.mult)
-    jv = V([kf, kb], vec.tensor_tensor, T.jv[:, :], T.fa[:, :], T.ib[:, :], A.add)
-    kh = V([kg, kt], vec.tensor_tensor, T.ut[:, :], T.fu[:, :], T.it[:, :], A.add)
-    lr = V([kh, i3], vec.tensor_scalar, T.lrn[:, :], T.iw[:, :], T.ut[:, :], None, A.add)
-
-    pl1 += [S([d1], act, T.c1p[:, K * t:K * (t + 1)], T.c1t[:, t:4 * K:4], FN.Copy) for t in (2, 3)]
+    lm = V([], vec.memset, T.lim[:, :], LOW)
+    gz = V([], vec.memset, T.gl[:, :], 0.0)
 
     score_no = [0]
 
-    def scan(b, dep):
+    def last(k):
+        return T.run[:, K * (k + 1) - 1:K * (k + 1)]
+
+    def scan(b, dep, on=None):
         k = score_no[0]
         score_no[0] += 1
-        tk = V([dep, lm], vec.tensor_tensor_scan, T.run[:, K * k:K * (k + 1)], bank[b][:, 0:K], T.lim[:, :], LOW, A.max, A.max)
+        tk = V([dep, lm] + ([on] if on else []), vec.tensor_tensor_scan, T.run[:, K * k:K * (k + 1)], bank[b][:, 0:K], T.lim[:, :],
+               last(k - 1) if on else LOW, A.max, A.max)
         free[b] = [tk]
         return k, tk
 
-    def sign(k, tk, acc):
-        return S([tk], act, T.junk[:, K * k:K * (k + 1)], T.run[:, K * k:K * (k + 1)], FN.Sign,
-                 bias=T.run[:, K * (k + 1) - 1:K * (k + 1)], scale=-1.0, accum_out=acc)
+    def sign(k, n, deps, acc):
+        a, b = K * (k + 1 - n), K * (k + 1)
+        return S(deps, act, T.junk[:, a:b], T.run[:, a:b], FN.Sign, bias=last(k), scale=-1.0, accum_out=acc)
 
-    so = mm(4, K, T.xqc, T.xqs, m0, T.q1c, T.q1s, 0, [qx, q1])
-    to = [mm(b, K, T.eqc, T.eqs, 128 * b, T.q1c, T.q1s, 0, [qe, q1]) for b in range(4)]
-    k0, s0 = scan(4, so)
-    n0 = sign(k0, s0, T.sci1[:, 4 * me + 1:4 * me + 2])
-    ow = [V([s0], vec.tensor_copy, T.sci1[:, 4 * me:4 * me + 1], T.run[:, K * (k0 + 1) - 1:K * (k0 + 1)])]
+    def lists(z, n, of, r0, deps):
+        gl, wl, ol = 32 * z, 4 * z, 64 * z
+        a = [V(deps + [gz], vec.tensor_copy, T.gl[0:32, gl + c:gl + 4 * n:4], T.gl[32 * c:32 * (c + 1), gl:gl + 4 * n:4])
+             for c in (1, 2, 3)]
+        b = [V(a, vec.transpose, T.wl[0:32, wl + 2 * e:wl + 2 * e + 2, :], T.gl[0:32, gl:gl + 32]) for e in (0, 1)]
+        d = [V(b, vec.transpose, T.ol[0:32, ol + h:ol + 64:2], T.wl[0:32, wl + h:wl + 4:2, :]) for h in (0, 1)]
+        return b[0], [V(d, vec.tensor_copy, of[32 * c:32 * (c + 1), 0:8 * (n - r0)], T.ol[0:32, ol + 8 * r0:ol + 8 * n]) for c in range(4)]
+
+    pl = {}
+
+    def planes(slot):
+        for st in PLANES[slot]:
+            win, src, dep = (T.c1p, T.c1t, d1) if st[0] == "1" else (T.c2p, T.c2t, d2)
+            t = int(st[1])
+            o, i = win[:, K * t:K * (t + 1)], src[:, t:4 * K:4]
+            if st[2] == "g":
+                pl[st[:2]] = G([dep], g.affine_select, o, i, [[0, K]], A.is_ge, 0.0, 0, 0)
+            else:
+                pl[st[:2]] = V([dep], vec.tensor_copy, o, i) if st[2] == "v" else S([dep], act, o, i, FN.Copy)
+
     t1 = [[], [], [], []]
-    for b in range(4):
-        t1[b] += evac("v" if b < 2 else "s", b, K, T.tab1, W1, b, [(0, base1[me], K)], to[b])
-    hm = K * home.index(me)
-    q2 = V([d2], vec.quantize_mx, T.q2c[:, hm:hm + K], T.q2s[:, hm:hm + K], T.c2t[:, :])
-    send([q2], "ac2", [(mates, u8(T.q2c, hm, hm + K), u8(T.q2c, hm, hm + K))])
-    send([q2], "ac2", [(mates, T.q2s[:, hm:hm + K], T.q2s[:, hm:hm + K])])
-    wz = V([], vec.memset, T.wp1[:, :], 0.0)
-    nz = V([], vec.memset, T.nc[:, :], 0.0)
-    p1 = []
-    for q in others:
-        p1.append(V([jv], vec.tensor_scalar, T.pp1[:, q:q + 1], T.jv[:, :], float(base1[q]), None, A.add))
-    xv = S([u0, u1, lr], act, T.xv[:, :], T.xs[:, 0:512].indirect(T.lrn[:, 0:32]), FN.Copy)
-
-    def score(group, banks, rc, rs, qc, qs, arrived, dw):
-        return [mm(banks[i], K, rc, rs, 128 * q, qc, qs, dw, [arrived(q)]) for i, q in enumerate(group)]
-
-    def search(group, banks, tks, mi):
-        n = len(group)
-        sc = [scan(banks[i], tks[i]) for i in range(n)]
-        first = sc[0][0]
-        mx = V([s for _, s in sc], vec.tensor_copy, mi[:, 0:2 * n:2], T.run[:, K * (first + 1) - 1:K * (first + n):K])
-        sg = [sign(k, tk, mi[:, 2 * i + 1:2 * i + 2]) for i, (k, tk) in enumerate(sc)]
-        return [mx] + sg
-
-    def spread(name, src, dst, deps, queues):
-        for k in range(8):
-            D(queues[k % len(queues)], deps, name, dst[16 * k:16 * (k + 1), :], src[:, :])
-        return (name, total[name])
-
-    def relist(n, cv, of, dep):
-        return [V([dep], vec.tensor_copy, of[:, 8 * k:8 * (k + 1)], cv[:, 2 * k + 1:16 * n:2 * n]) for k in range(n)]
-
-    def gather(n, of, win, gt, deps):
-        tk = []
-        for t in (0, 1):
-            tk.append(V(deps, vec.tensor_copy, gt[:, t:512 * n:4], win[:, K * t:K * (t + 1)].indirect(of[:, 0:8 * n])))
-        for t in (2, 3):
-            tk.append(S(deps, act, gt[:, t:512 * n:4], win[:, K * t:K * (t + 1)].indirect(of[:, 0:8 * n]), FN.Copy))
-        return tk
-
-    def give(group, cc, cs, dep, name, kc, ks, slot):
-        send([dep], name, [([q], u8(cc, 128 * i, 128 * (i + 1)), u8(kc, 128 * slot(q), 128 * (slot(q) + 1)))
-                           for i, q in enumerate(group)])
-        send([dep], name, [([q], cs[:, 128 * i:128 * (i + 1)], ks[:, 128 * slot(q):128 * (slot(q) + 1)])
-                           for i, q in enumerate(group)])
-
-    def tell(group, mi, deps, name, sci):
-        send(deps, name, [([q], mi[:, 2 * i:2 * i + 2], sci[:, 4 * me:4 * me + 2]) for i, q in enumerate(group)])
-
-    def slot_a(q):
-        return mates_of(q).index(me)
-
-    def slot_b(q):
-        return far_of(q).index(me)
-
-    wx = 2 * width(1)
-    ma = score(mates, [5, 6, 7], T.xqc, T.xqs, T.q1c, T.q1s, lambda q: ("ax%d" % q, wx), 0)
-    mb = score(far, [0, 1, 2, 3], T.xqc, T.xqs, T.q1c, T.q1s, lambda q: ("ax%d" % q, wx), 0)
-    sa = search(mates, [5, 6, 7], ma, T.mia)
-    ca = spread("cva", T.mia, T.cva, sa, ["y"])
-    tell(mates, T.mia, sa, "as1", T.sci1)
-    sbt = search(far, [0, 1, 2, 3], mb, T.mib)
-    cb = spread("cvb", T.mib, T.cvb, sbt, ["y", "s"])
-    tell(far, T.mib, sbt, "as1", T.sci1)
-    la = relist(3, T.cva, T.ofa, ca)
-    ga = gather(3, T.ofa, T.c1p, T.gta, la + pl1)
-    qa = V(ga, vec.quantize_mx, T.sac[:, :], T.sas[:, :], T.gta[:, :])
-    give(mates, T.sac, T.sas, qa, "aka", T.kac, T.kas, slot_a)
-    lb = relist(4, T.cvb, T.ofb, cb)
-    gb = gather(4, T.ofb, T.c1p, T.gtb, lb + pl1)
-    qb = V(gb, vec.quantize_mx, T.sbc[:, :], T.sbs[:, :], T.gtb[:, :])
-    give(far, T.sbc, T.sbs, qb, "akb", T.kbc, T.kbs, slot_b)
-
-    def choose(sci, pen, tp, pp, pos, mxo, deps):
-        sc = sci[:, 0:32:4]
-        a = V(deps, vec.tensor_reduce, mxo, sc, X, A.max)
-        b = V([a], vec.tensor_scalar, pen[:, :], sc, mxo, BIG, A.is_lt, A.mult)
-        c = V([b], vec.tensor_tensor, tp[:, :], pen[:, :], pp[:, :], A.add)
-        return a, b, V([c], vec.tensor_reduce, pos[:, :], tp[:, :], X, A.min)
-
-    def number(sci, num, pen, tn, wo, deps):
-        a = V(deps, vec.tensor_tensor, num[:, :], sci[:, 1:32:4], T.nb[:, :], A.add)
-        b = V([a], vec.tensor_tensor, tn[:, :], pen[:, :], num[:, :], A.add)
-        return V([b], vec.tensor_reduce, wo, tn[:, :], X, A.min)
-
-    po = V([n0, jv], vec.tensor_scalar, T.pp1[:, me:me + 1], T.sci1[:, 4 * me + 1:4 * me + 2], float(base1[me]), None, A.add)
-    w4 = width(3)
-    ars1 = ("as1", 3 * width(3) + 4 * width(4))
-    c1a, c1b, c1c = choose(T.sci1, T.pen1, T.tp1, T.pp1, T.pos1, T.wp1[:, 1:2], [ars1, po, n0, wz] + p1 + ow)
-    cp1 = spread("cvp1", T.pos1, T.cvp1, [c1c], ["y"])
-
-    to2 = [mm(4 + b, K, T.eqc, T.eqs, 128 * b, T.q2c, T.q2s, hm, [q2, qe]) for b in range(4)]
     t2 = [[], [], [], []]
+    lent = ("ac", 3 * 2 * width(1))
 
-    def mate_table(b0, q, tks):
-        for b in range(4):
-            t2[b] += evac("v" if b < 2 else "s", b0 + b, K, T.tab2, W2, b, [(0, base2[q], K)], tks[b])
+    def held(slot, banks):
+        todo = [((place + int(st[0])) % 4, int(st[1]), st[2]) for st in HELD[slot]]
+        for a in range(0, len(todo), len(banks)):
+            part = list(zip(todo[a:a + len(banks)], banks))
+            tk = [unpack(b, t, K, T.q2c, T.q2s, K * k, q2 if k == place else lent) for (k, t, _), b in part]
+            for ((k, t, who), b), d in zip(part, tk):
+                t2[t].append(evac(who, b, K, T.tab2, W2 * t + K * k, d))
 
-    mate_table(4, me, to2)
-    da = [mm(b, 384, T.eqc, T.eqs, 128 * b, T.kac, T.kas, 0, [("aka", 2 * 3 * width(3)), qe]) for b in range(4)]
-    pl2 = [V([d2], vec.tensor_copy, T.c2p[:, K * t:K * (t + 1)], T.c2t[:, t:4 * K:4]) for t in (0, 1)]
-    pl2 += [S([d2], act, T.c2p[:, K * t:K * (t + 1)], T.c2t[:, t:4 * K:4], FN.Copy) for t in (2, 3)]
-    ra = runs_of(mates, base1)
-    for b in range(4):
-        t1[b] += evac("v" if b < 2 else "s", b, 384, T.tab1, W1, b, ra, da[b])
-    nu1 = number(T.sci1, T.num1, T.pen1, T.tn1, T.wp1[:, 0:1], [ars1, n0, i4, c1b, wz])
-    wt = V([nu1, c1a], vec.transpose, T.wt1[:, :], T.wp1[:, :])
-    of1 = V([cp1], vec.tensor_copy, T.ofp1[:, :], T.cvp1[:, :])
+    h0 = K * place
+    q1 = V([d1], vec.quantize_mx, T.q1c[:, :], T.q1s[:, :], T.c1t[:, :])
+    q2 = V([d2], vec.quantize_mx, T.q2c[:, h0:h0 + K], T.q2s[:, h0:h0 + K], T.c2t[:, :])
+    so = mm(4, K, T.xqc, T.xqs, m0, T.q1c, T.q1s, 0, [qx, q1])
+    to = [unpack(t, t, K, T.q1c, T.q1s, 0, q1) for t in range(4)]
+    planes("early")
+    send([q2], "ac", [(near_out, u8(T.q2c, h0, h0 + K), u8(T.q2c, h0, h0 + K))])
+    send([q2], "ac", [(near_out, T.q2s[:, h0:h0 + K], T.q2s[:, h0:h0 + K])])
+    planes("lent")
+    k0, s0 = scan(4, so)
+    for t in range(4):
+        t1[t].append(evac("ssvv"[t], t, K, T.tab1, W1 * t, to[t]))
+    n0 = sign(k0, 1, [s0], T.pp1[:, 7:8])
+    ow = [n0, S([s0], act, T.sci1[:, 28:29], last(k0), FN.Copy),
+          S([n0], act, T.sci1[:, 29:30], T.pp1[:, 7:8], FN.Identity, bias=float(K * me))]
+    held("early", [5, 6, 7, 4])
 
-    db = [mm(4 + b, 512, T.eqc, T.eqs, 128 * b, T.kbc, T.kbs, 0, [("akb", 2 * 4 * width(4)), qe]) for b in range(4)]
-    rb = runs_of(far, base1)
-    for b in range(4):
-        t1[b] += evac("v" if b < 1 else "s", 4 + b, 512, T.tab1, W1, b, rb, db[b])
-    rr = [V([of1, xv] + t1[t], vec.tensor_tensor, T.rt[:, t:512:4], T.tab1[:, W1 * t:W1 * (t + 1)].indirect(T.ofp1[:, 0:8]),
-            T.xv[:, t:512:4], A.add) for t in range(4)]
+    def search(group, banks, rc, rs, qc, qs, a, name, z, mi, sci, told):
+        n = len(group)
+        tk = [mm(banks[i], K, rc, rs, 128 * q, qc, qs, a, [(name % q, 2 * width(1))]) for i, q in enumerate(group)]
+        sc = [scan(banks[i], tk[i]) for i in range(n)]
+        sg = [sign(k, 1, [s, gz], T.gl[:, 32 * z + 4 * i:32 * z + 4 * i + 1]) for i, (k, s) in enumerate(sc)]
+        first = sc[0][0]
+        a = S([s for _, s in sc], act, mi[:, 0:2 * n:2], T.run[:, K * (first + 1) - 1:K * (first + n):K], FN.Copy)
+        b = S(sg, act, mi[:, 1:2 * n:2], T.gl[:, 32 * z:32 * z + 4 * n:4], FN.Identity, bias=float(K * me))
+        send([a, b], told, [([q], mi[:, 2 * i:2 * i + 2], sci[:, 4 * i:4 * i + 2]) for i, q in enumerate(group)])
+        return sg
+
+    def answer(group, sizes, steps, of, win, book, gt, cc, cs, kc, ks, name, deps):
+        made = [[] for _ in sizes]
+        for st in steps:
+            b = int(st[0])
+            a, n = cuts(sizes)[b]
+            if len(st) > 1:
+                t = int(st[1])
+                o, i = gt[:, 512 * a + t:512 * (a + n):4], win[:, K * t:K * (t + 1)].indirect(of[:, 8 * a:8 * (a + n)])
+                d = deps + [pl[book + st[1]]]
+                made[b].append(V(d, vec.tensor_copy, o, i) if st[2] == "v" else S(d, act, o, i, FN.Copy))
+                continue
+            tk = V(made[b], vec.quantize_mx, cc[:, 128 * a:128 * (a + n)], cs[:, 128 * a:128 * (a + n)], gt[:, 512 * a:512 * (a + n)])
+            send([tk], name % b, [([group[k]], u8(cc, 128 * k, 128 * (k + 1)), u8(kc, 128 * k, 128 * (k + 1))) for k in range(a, a + n)])
+            send([tk], name % b, [([group[k]], cs[:, 128 * k:128 * (k + 1)], ks[:, 128 * k:128 * (k + 1)]) for k in range(a, a + n)])
+
+    def receive(b, banks, sizes, who, kc, ks, name, tab, w, base, tt):
+        a, n = cuts(sizes)[b]
+        tk = [unpack(banks[t], t, 128 * n, kc, ks, 128 * a, (name % b, 2 * n * width(n))) for t in range(4)]
+        for t in range(4):
+            tt[t].append(evac(who[b][t], banks[t], 128 * n, tab, w * t + base + 128 * a, tk[t]))
+
+    sg1 = search(in1, [0, 1, 2, 3, 5, 6, 7], T.xqc, T.xqs, T.q1c, T.q1s, 0, "ax%d", 0, T.mi1, T.sci1, "as1")
+    held("list1", EVEN)
+    _, l1 = lists(0, 7, T.of1, 0, sg1)
+    answer(in1, BACK1, STEPS1, T.of1, T.c1p, "1", T.gt1, T.s1c, T.s1s, T.k1c, T.k1s, "k1%d", l1)
+    planes("wait2")
+
+    def choose(sci, n, ch, pp, top, no, pos, deps):
+        sc = sci[:, 0:4 * n:4]
+        a = V(deps, vec.tensor_reduce, top, sc, X, A.max)
+        b = V([a], vec.tensor_scalar, ch[:, 0:n], sc, top, BIG, A.is_lt, A.mult)
+        c = V([b], vec.tensor_tensor, ch[:, 8:8 + n], ch[:, 0:n], sci[:, 1:4 * n:4], A.add)
+        d = V([c], vec.tensor_reduce, no, ch[:, 8:8 + n], X, A.min)
+        e = V([d], vec.tensor_scalar, ch[:, 16:16 + n], ch[:, 8:8 + n], no, BIG, A.is_gt, A.mult)
+        f = V([e], vec.tensor_tensor, ch[:, 24:24 + n], ch[:, 16:16 + n], pp[:, 0:n], A.add)
+        return V([f], vec.tensor_reduce, pos, ch[:, 24:24 + n], X, A.min)
+
+    def col(c):
+        return T.gl[:, c:c + 1]
+
+    NO = 96
+    held("wait2", ODD)
+    c1 = choose(T.sci1, 8, T.ch1, T.pp1, col(NO + 8), col(NO), col(32), [("as1", 7 * width(7)), gz, p1] + ow)
+    _, lp1 = lists(1, 1, T.op1, 0, [c1])
+    for b in range(len(BACK1)):
+        receive(b, [EVEN, ODD][b % 2], BACK1, EVAC1, T.k1c, T.k1s, "k1%d", T.tab1, W1, K, t1)
+    rr = [V(lp1 + [dx] + t1[t], vec.tensor_tensor, T.rt[:, t:512:4], T.tab1[:, W1 * t:W1 * (t + 1)].indirect(T.op1[:, 0:8]),
+            T.xt[:, t:512:4], A.add) for t in range(4)]
     qr = V(rr, vec.quantize_mx, T.rqc[:, m0:m0 + 128], T.rqs[:, m0:m0 + 128], T.rt[:, :])
-    send([qr], "ar%d" % me, [(far, u8(T.rqc, m0, m0 + 128), u8(T.rqc, m0, m0 + 128))])
-    send([qr], "ar%d" % me, [(far, T.rqs[:, m0:m0 + 128], T.rqs[:, m0:m0 + 128])])
+    spread(qr, "ar%d" % me, T.rqc, T.rqs, m0, m0 + 128, out2, OUT2)
+    planes("wait3")
 
-    ac2 = ("ac2", 3 * 2 * width(1))
-    ml = [mm(i, K, T.rqc, T.rqs, m0, T.q2c, T.q2s, K * i, [qr, q2, ac2]) for i in range(4)]
-    m1 = [mm(4 + b, K, T.eqc, T.eqs, 128 * b, T.q2c, T.q2s, K * home.index(mates[0]), [ac2, qe]) for b in range(4)]
-    sl = [scan(i, ml[i]) for i in range(4)]
+    tk = [mm(EVEN[k], K, T.rqc, T.rqs, m0, T.q2c, T.q2s, K * k, [qr, q2, lent]) for k in range(4)]
     lo = []
-    for (k, tk), q in zip(sl, home):
-        lo.append(sign(k, tk, T.sci2[:, 4 * q + 1:4 * q + 2]))
-    for (k, tk), q in zip(sl, home):
-        lo.append(V([tk], vec.tensor_copy, T.sci2[:, 4 * q:4 * q + 1], T.run[:, K * (k + 1) - 1:K * (k + 1)]))
-    rn = S(rr + [lr], act, T.rn[:, :], T.rt[:, 0:512].indirect(T.lrn[:, 0:32]), FN.Copy)
-    mate_table(4, mates[0], m1)
-    il = [D("y", [wt], "il", T.il[0:1, 128 * c:128 * (c + 1)], T.wt1[c:128:32, 0:32]) for c in range(2)]
-    mc = score(far, [0, 1, 2, 3], T.rqc, T.rqs, T.q2c, T.q2s, lambda q: ("ar%d" % q, wx), hm)
-    sct = search(far, [0, 1, 2, 3], mc, T.mic)
-    cc = spread("cvc", T.mic, T.cvc, sct, ["y", "s"])
-    tell(far, T.mic, sct, "as2", T.sci2)
-    m2 = [mm(4 + b, K, T.eqc, T.eqs, 128 * b, T.q2c, T.q2s, K * home.index(mates[1]), [ac2, qe]) for b in range(4)]
-    mate_table(4, mates[1], m2)
-    lc = relist(4, T.cvc, T.ofc, cc)
-    gc = gather(4, T.ofc, T.c2p, T.gtc, lc + pl2)
-    qc = V(gc, vec.quantize_mx, T.scc[:, :], T.scs[:, :], T.gtc[:, :])
-    give(far, T.scc, T.scs, qc, "akc", T.kcc, T.kcs, slot_b)
+    for h in (0, 1):
+        _, s = scan(EVEN[2 * h], tk[2 * h])
+        k, s = scan(EVEN[2 * h + 1], tk[2 * h + 1], s)
+        n = sign(k, 2, [s], T.ix[:, h:h + 1])
+        lo += [S([s], act, T.sci2[:, 16 + 4 * h:17 + 4 * h], last(k), FN.Copy),
+               S([n], act, T.sci2[:, 17 + 4 * h:18 + 4 * h], T.ix[:, h:h + 1], FN.Identity, bias=float(K * home[2 * h])),
+               S([n], act, T.pp2[:, 4 + h:5 + h], T.ix[:, h:h + 1], FN.Identity, bias=float(2 * K * h))]
+    held("wait3", ODD)
+    sg2 = search(in2, ODD, T.rqc, T.rqs, T.q2c, T.q2s, h0, "ar%d", 2, T.mi2, T.sci2, "as2")
+    held("list2", EVEN)
+    _, l2 = lists(2, 4, T.of2, 0, sg2)
+    answer(in2, BACK2, STEPS2, T.of2, T.c2p, "2", T.gt2, T.s2c, T.s2s, T.k2c, T.k2s, "k2%d", l2)
 
-    p2 = []
-    for q in ranks:
-        if q in home:
-            p2.append(V(lo, vec.tensor_scalar, T.pp2[:, q:q + 1], T.sci2[:, 4 * q + 1:4 * q + 2], float(base2[q]), None, A.add))
-        else:
-            p2.append(V([jv], vec.tensor_scalar, T.pp2[:, q:q + 1], T.jv[:, :], float(base2[q]), None, A.add))
-    ars2 = ("as2", 4 * width(4))
-    c2a, c2b, c2c = choose(T.sci2, T.pen2, T.tp2, T.pp2, T.pos2, T.wp2[:, 1:2], [ars2] + p2 + lo)
-    cp2 = spread("cvp2", T.pos2, T.cvp2, [c2c], ["y"])
-    nu2 = number(T.sci2, T.num2, T.pen2, T.tn2, T.wp2[:, 0:1], [ars2, i4, c2b] + lo)
-    m3 = [mm(b, K, T.eqc, T.eqs, 128 * b, T.q2c, T.q2s, K * home.index(mates[2]), [ac2, qe]) for b in range(4)]
-    mate_table(0, mates[2], m3)
-    dn = D("y", [nu2, c2a, nz], "nc", T.nc[0:16, 0:16], T.wp2[:, :])
-    ov = [V([il[1]], vec.tensor_copy, T.ou[0:1, 128 * c + h:128 * (c + 1):2], T.il[0:1, 128 * c + 64 * h:128 * c + 64 * (h + 1)])
-          for c in range(2) for h in range(2)]
-    D("y", ov, "no1", T.no[0:3:2, :], T.ou[0:1, :])
-    of2 = V([cp2], vec.tensor_copy, T.ofp2[:, :], T.cvp2[:, :])
-    nt = V([dn], vec.transpose, T.nct[0:32, :], T.nc[0:32, :])
-    D("y", [nt], "no2", T.no[1, :], T.nct[0:16:2, 0:16])
-    D("y", [nt], "no2", T.no[3, :], T.nct[1:16:2, 0:16])
-
-    dc = [mm(4 + b, 512, T.eqc, T.eqs, 128 * b, T.kcc, T.kcs, 0, [("akc", 2 * 4 * width(4)), qe]) for b in range(4)]
-    rc = runs_of(far, base2)
-    for b in range(4):
-        t2[b] += evac("v" if b < 1 else "s", 4 + b, 512, T.tab2, W2, b, rc, dc[b])
-    yy = [V([of2, rn] + t2[t], vec.tensor_tensor, T.yt[:, t:512:4], T.tab2[:, W2 * t:W2 * (t + 1)].indirect(T.ofp2[:, 0:8]),
-            T.rn[:, t:512:4], A.add) for t in range(4)]
-    D("y", yy, "yo", T.y[:, :], T.yt[:, :])
+    held("wait4", ODD)
+    c2 = choose(T.sci2, 6, T.ch2, T.pp2, col(NO + 12), col(NO + 4), col(NO + 16), [("as2", 4 * width(4)), p2] + lo)
+    nt, lp2 = lists(3, 5, T.op2, 4, [c2])
+    D("y", [nt], "no", T.no[:, :], T.wl[0:16, 12:14, :])
+    for b in range(len(BACK2)):
+        receive(b, [EVEN, ODD][b % 2], BACK2, EVAC2, T.k2c, T.k2s, "k2%d", T.tab2, W2, 4 * K, t2)
+    for a, n in cuts(STORE):
+        yy = [V(lp2 + rr + t2[t], vec.tensor_tensor, T.yt[:, 64 * a + t:64 * (a + n):4],
+                T.tab2[:, W2 * t:W2 * (t + 1)].indirect(T.op2[:, a:a + n]), T.rt[:, 64 * a + t:64 * (a + n):4], A.add) for t in range(4)]
+        D("y", yy, "yo", T.y[:, 64 * a:64 * (a + n)], T.yt[:, 64 * a:64 * (a + n)])
 
     need("g", [(n, count[n]) for n in count] + [("ls", local[0])])
     need("y", [(n, total[n]) for n in total])

@@ -7,14 +7,16 @@ W2 = 4 * K + 4 * 128
 BIG = 1000000.0
 LOW = -9.0e29
 
-OUT1, OUT2 = [3, 4], [4]
+OUT1, OUT2 = [("s", 0, 7, (0, 2)), ("c", 0, 2, (1, 2)), ("c", 2, 7, (0, 1))], [("s", 0, 4, (0, 1)), ("c", 0, 4, (0, 1))]
 BACK1, BACK2 = [4, 3], [2, 2]
-STEPS1 = ["00v", "02s", "01v", "03s", "0", "11s", "10v", "12s", "13s", "1"]
-STEPS2 = ["00v", "02s", "01v", "03s", "0", "11s", "12s", "10v", "13v", "1"]
-EVAC1, EVAC2 = ["vvss", "vsvs"], ["vsss", "vsvs"]
-HELD = {"early": ["00v", "01s", "02s", "03s"], "list1": [], "wait2": ["10s", "11s", "12s", "13s", "20s", "21s"], "wait3": [], "list2": ["30s", "31s"], "wait4": ["32s", "33s", "22s", "23s"]}
-PLANES = {"early": [], "lent": ["10g", "11g", "12g", "13g"], "wait2": ["20g", "21g"], "wait3": ["22g", "23g"]}
-STORE = [4, 4]
+LISTS1 = [7]
+LISTS2 = [4]
+STEPS1 = "s0 s1 s2 s3 s4 s5 s6 n0 n1 n2 n3 n4 n5 n6 t h L0 g00v g02s g01v g03s q0 g11s g12s g10v g13v q1 c"
+STEPS2 = "s0 s1 s2 s3 n0 n1 n2 n3 t b h L0 g00v g02s g01v g03s q0 g11s g12s d g10v g13v q1 c"
+EVAC1, EVAC2 = [["0v", "1s", "2s", "3s"], ["0v", "1s", "2v02", "2s21", "3s"]], [["0v", "1s", "2s", "3s"], ["0v", "1s", "2s", "3s"]]
+HELD = {"first": ["a0s", "a1s", "a2v", "a3v"], "early": ["01s"], "list1": ["02v", "03s", "00s"], "wait2": ["10s", "11s", "12s", "13s", "20s"], "pick1": ["21s", "22s", "23s"], "wait3": ["30s"], "list2": ["31v"], "wait4": ["32s", "33s"]}
+PLANES = {"early": ["13s"], "lent": ["10g", "11g", "12g"], "wait2": ["20g", "21g"], "wait3": ["22g", "23g"]}
+STORE = [8]
 
 F, B, C8, U8, I32, U16 = "float32", "bfloat16", "float8_e4m3fn_x4", "uint8", "int32", "uint16"
 
@@ -25,11 +27,11 @@ def sb(n, d):
 
 SCRATCH = {
     "xt": sb(512, B), "c1t": sb(4 * K, B), "c2t": sb(4 * K, B), "c1p": sb(4 * K, B), "c2p": sb(4 * K, B),
-    "ones": sb(128, B), "ident": sb(128, B), "et": sb(2048, B), "eqc": sb(512, C8), "eqs": sb(512, U8), "lim": sb(K, B),
+    "ones": sb(K, B), "ident": sb(128, B), "et": sb(516, B), "eqc": sb(512, C8), "eqs": sb(512, U8),
     "xqc": sb(1024, C8), "xqs": sb(1024, U8), "rqc": sb(1024, C8), "rqs": sb(1024, U8),
     "q1c": sb(K, C8), "q1s": sb(K, U8), "q2c": sb(4 * K, C8), "q2s": sb(4 * K, U8),
     "run": sb(16 * K, F), "junk": sb(16 * K, B),
-    "gl": sb(128, F), "wl": ("sbuf", [128, 16, 16], F), "ol": sb(256, F),
+    "gl": sb(192, F), "wl": ("sbuf", [128, 24, 16], F), "ol": sb(384, F),
     "mi1": sb(16, F), "mi2": sb(8, F), "of1": sb(56, U16), "of2": sb(32, U16), "op1": sb(8, U16), "op2": sb(8, U16),
     "gt1": sb(7 * 512, B), "gt2": sb(4 * 512, B),
     "s1c": sb(896, C8), "s1s": sb(896, U8), "s2c": sb(512, C8), "s2s": sb(512, U8),
@@ -59,9 +61,10 @@ def rank_program(g, core, T, topo):
     def turn(group, k):
         return group[(place + k) % len(group)]
 
-    out2, in2 = [turn(far, k) for k in range(4)], [turn(far, -k) for k in range(4)]
+    out2 = in2 = [far[place ^ k] for k in range(4)]
     near_out, near_in = [turn(home, k) for k in (1, 2, 3)], [turn(home, -k) for k in (1, 2, 3)]
     out1, in1 = out2 + near_out, in2 + near_in
+    at_held, at_road = (0, 4 * K) if home[0] < far[0] else (4 * 128, 0)
     sem = T.sem
     queue = {"v": g.vector, "s": g.scalar, "t": g.tensor, "g": g, "y": g.sync}
     count, seen, local, total = {}, {}, [0], {}
@@ -107,14 +110,14 @@ def rank_program(g, core, T, topo):
             k *= 2
         return len(engines) // k
 
-    def send(deps, name, items):
+    def send(deps, name, items, part=(0, 1)):
         need("g", deps)
-        per = width(len(items))
+        per = width(len(items)) // part[1]
         step = len(engines) // per
         tr = []
         for k, (dst, s, d) in enumerate(items):
             mask = 0
-            for e in engines[k::step]:
+            for e in engines[k + part[0]::step]:
                 mask |= 1 << e
             ids = []
             for q in dst:
@@ -131,9 +134,12 @@ def rank_program(g, core, T, topo):
         return [(sum(sizes[:b]), n) for b, n in enumerate(sizes)]
 
     def spread(dep, name, qc, qs, a, b, dst, sizes):
-        for i, n in cuts(sizes):
-            send([dep], name, [(dst[i:i + n], qs[:, a:b], qs[:, a:b])])
-            send([dep], name, [(dst[i:i + n], u8(qc, a, b), u8(qc, a, b))])
+        for kind, i, j, part in sizes:
+            v = qs[:, a:b] if kind == "s" else u8(qc, a, b)
+            send([dep], name, [(dst[i:j], v, v)], part)
+
+    def landed(sizes, k):
+        return sum(len(engines) // part[1] for _, i, j, part in sizes if i <= k < j)
 
     bank = [T["p%d" % b] for b in range(8)]
     free = [[] for _ in range(8)]
@@ -145,7 +151,7 @@ def rank_program(g, core, T, topo):
                                             rc[:, ra:ra + n], rsc[:, ra:ra + n], True, True))
 
     def unpack(b, t, n, qc, qs, a, dep):
-        return mm(b, n, T.eqc, T.eqs, 128 * t, qc, qs, a, [dep, qe])
+        return mm(b, n, T.eqc, T.eqs, 128 * t, qc, qs, a, [dep, qe[t]])
 
     def evac(qn, b, n, tab, a, dep):
         o, i = tab[:, a:a + n], bank[b][:, 0:n]
@@ -161,18 +167,18 @@ def rank_program(g, core, T, topo):
     d2 = D("y", [], "lc2", T.c2t[:, :], T.c2[:, :])
 
     o1 = V([], vec.memset, T.ones[:, :], 1.0)
-    i1 = G([o1], g.affine_select, T.ident[:, :], T.ones[:, :], [[-1, 128]], A.is_equal, 0.0, 0, 1)
+    i1 = G([o1], g.affine_select, T.ident[:, :], T.ones[:, 0:128], [[-1, 128]], A.is_equal, 0.0, 0, 1)
     p1 = G([], g.iota, T.pp1[:, 0:7], [[128, 7]], K, 1, allow_small_or_imprecise_dtypes=True)
-    p2 = G([], g.iota, T.pp2[:, 0:4], [[128, 4]], 4 * K, 1, allow_small_or_imprecise_dtypes=True)
+    p2 = G([], g.iota, T.pp2[:, 0:4], [[128, 4]], at_road, 1, allow_small_or_imprecise_dtypes=True)
+    gz = G([], g.iota, T.gl[:, 0:128], [[0, 128]], 0, 0, allow_small_or_imprecise_dtypes=True)
     ez = V([], vec.memset, T.et[:, :], 0.0)
-    ec = [V([i1, ez], vec.tensor_copy, T.et[:, 512 * b + b:512 * (b + 1):4], T.ident[:, :]) for b in range(4)]
+    ec = V([i1, ez], vec.tensor_copy, T.et[:, 3:515:4], T.ident[:, :])
+    qe = [V([ec], vec.quantize_mx, T.eqc[:, 128 * b:128 * (b + 1)], T.eqs[:, 128 * b:128 * (b + 1)], T.et[:, 3 - b:515 - b])
+          for b in range(4)]
 
     m0 = 128 * me
     qx = V([dx], vec.quantize_mx, T.xqc[:, m0:m0 + 128], T.xqs[:, m0:m0 + 128], T.xt[:, :])
     spread(qx, "ax%d" % me, T.xqc, T.xqs, m0, m0 + 128, out1, OUT1)
-    qe = V(ec, vec.quantize_mx, T.eqc[:, :], T.eqs[:, :], T.et[:, :])
-    lm = V([], vec.memset, T.lim[:, :], LOW)
-    gz = V([], vec.memset, T.gl[:, :], 0.0)
 
     score_no = [0]
 
@@ -182,8 +188,8 @@ def rank_program(g, core, T, topo):
     def scan(b, dep, on=None):
         k = score_no[0]
         score_no[0] += 1
-        tk = V([dep, lm] + ([on] if on else []), vec.tensor_tensor_scan, T.run[:, K * k:K * (k + 1)], bank[b][:, 0:K], T.lim[:, :],
-               last(k - 1) if on else LOW, A.max, A.max)
+        tk = V([dep, o1] + ([on] if on else []), vec.tensor_tensor_scan, T.run[:, K * k:K * (k + 1)], bank[b][:, 0:K], T.ones[:, :],
+               last(k - 1) if on else LOW, A.max, A.mult)
         free[b] = [tk]
         return k, tk
 
@@ -191,13 +197,17 @@ def rank_program(g, core, T, topo):
         a, b = K * (k + 1 - n), K * (k + 1)
         return S(deps, act, T.junk[:, a:b], T.run[:, a:b], FN.Sign, bias=last(k), scale=-1.0, accum_out=acc)
 
-    def lists(z, n, of, r0, deps):
+    def lists(z, n, of, at, deps):
         gl, wl, ol = 32 * z, 4 * z, 64 * z
         a = [V(deps + [gz], vec.tensor_copy, T.gl[0:32, gl + c:gl + 4 * n:4], T.gl[32 * c:32 * (c + 1), gl:gl + 4 * n:4])
              for c in (1, 2, 3)]
         b = [V(a, vec.transpose, T.wl[0:32, wl + 2 * e:wl + 2 * e + 2, :], T.gl[0:32, gl:gl + 32]) for e in (0, 1)]
         d = [V(b, vec.transpose, T.ol[0:32, ol + h:ol + 64:2], T.wl[0:32, wl + h:wl + 4:2, :]) for h in (0, 1)]
-        return b[0], [V(d, vec.tensor_copy, of[32 * c:32 * (c + 1), 0:8 * (n - r0)], T.ol[0:32, ol + 8 * r0:ol + 8 * n]) for c in range(4)]
+        if z in (1, 3):
+            for c in (0, 1):
+                D("y", b, "no", T.no[z // 2 + 2 * c, :], T.wl[4 + 4 * c:8 + 4 * c, wl:wl + 2, :])
+            n = 1
+        return [V(d, vec.tensor_copy, of[32 * c:32 * (c + 1), at:at + 8 * n], T.ol[0:32, ol:ol + 8 * n]) for c in range(4)]
 
     pl = {}
 
@@ -216,73 +226,100 @@ def rank_program(g, core, T, topo):
     lent = ("ac", 3 * 2 * width(1))
 
     def held(slot, banks):
-        todo = [((place + int(st[0])) % 4, int(st[1]), st[2]) for st in HELD[slot]]
+        todo = HELD[slot]
         for a in range(0, len(todo), len(banks)):
-            part = list(zip(todo[a:a + len(banks)], banks))
-            tk = [unpack(b, t, K, T.q2c, T.q2s, K * k, q2 if k == place else lent) for (k, t, _), b in part]
-            for ((k, t, who), b), d in zip(part, tk):
-                t2[t].append(evac(who, b, K, T.tab2, W2 * t + K * k, d))
+            part = []
+            for st, b in zip(todo[a:a + len(banks)], banks):
+                t = int(st[1])
+                if st[0] == "a":
+                    part.append((t1[t], st[2], b, T.tab1, W1 * t, unpack(b, t, K, T.q1c, T.q1s, 0, q1)))
+                else:
+                    k = (place + int(st[0])) % 4
+                    part.append((t2[t], st[2], b, T.tab2, W2 * t + at_held + K * k,
+                                 unpack(b, t, K, T.q2c, T.q2s, K * k, q2 if k == place else lent)))
+            for tt, who, b, tab, at, tk in part:
+                tt.append(evac(who, b, K, tab, at, tk))
 
     h0 = K * place
     q1 = V([d1], vec.quantize_mx, T.q1c[:, :], T.q1s[:, :], T.c1t[:, :])
     q2 = V([d2], vec.quantize_mx, T.q2c[:, h0:h0 + K], T.q2s[:, h0:h0 + K], T.c2t[:, :])
     so = mm(4, K, T.xqc, T.xqs, m0, T.q1c, T.q1s, 0, [qx, q1])
-    to = [unpack(t, t, K, T.q1c, T.q1s, 0, q1) for t in range(4)]
     planes("early")
     send([q2], "ac", [(near_out, u8(T.q2c, h0, h0 + K), u8(T.q2c, h0, h0 + K))])
     send([q2], "ac", [(near_out, T.q2s[:, h0:h0 + K], T.q2s[:, h0:h0 + K])])
     planes("lent")
     k0, s0 = scan(4, so)
-    for t in range(4):
-        t1[t].append(evac("ssvv"[t], t, K, T.tab1, W1 * t, to[t]))
+    held("first", [0, 1, 2, 3])
     n0 = sign(k0, 1, [s0], T.pp1[:, 7:8])
     ow = [n0, S([s0], act, T.sci1[:, 28:29], last(k0), FN.Copy),
           S([n0], act, T.sci1[:, 29:30], T.pp1[:, 7:8], FN.Identity, bias=float(K * me))]
     held("early", [5, 6, 7, 4])
 
-    def search(group, banks, rc, rs, qc, qs, a, name, z, mi, sci, told):
+    def road(no, group, banks, name, sent, qc, qs, at, sizes, groups, steps, aside):
+        rc, rs = (T.xqc, T.xqs) if no == "1" else (T.rqc, T.rqs)
+        mi, sci, of, win, gt = T["mi" + no], T["sci" + no], T["of" + no], T["c%sp" % no], T["gt" + no]
+        cc, cs, kc, ks = T["s%sc" % no], T["s%ss" % no], T["k%sc" % no], T["k%ss" % no]
         n = len(group)
-        tk = [mm(banks[i], K, rc, rs, 128 * q, qc, qs, a, [(name % q, 2 * width(1))]) for i, q in enumerate(group)]
-        sc = [scan(banks[i], tk[i]) for i in range(n)]
-        sg = [sign(k, 1, [s, gz], T.gl[:, 32 * z + 4 * i:32 * z + 4 * i + 1]) for i, (k, s) in enumerate(sc)]
-        first = sc[0][0]
-        a = S([s for _, s in sc], act, mi[:, 0:2 * n:2], T.run[:, K * (first + 1) - 1:K * (first + n):K], FN.Copy)
-        b = S(sg, act, mi[:, 1:2 * n:2], T.gl[:, 32 * z:32 * z + 4 * n:4], FN.Identity, bias=float(K * me))
-        send([a, b], told, [([q], mi[:, 2 * i:2 * i + 2], sci[:, 4 * i:4 * i + 2]) for i, q in enumerate(group)])
-        return sg
-
-    def answer(group, sizes, steps, of, win, book, gt, cc, cs, kc, ks, name, deps):
-        made = [[] for _ in sizes]
-        for st in steps:
-            b = int(st[0])
-            a, n = cuts(sizes)[b]
-            if len(st) > 1:
-                t = int(st[1])
-                o, i = gt[:, 512 * a + t:512 * (a + n):4], win[:, K * t:K * (t + 1)].indirect(of[:, 8 * a:8 * (a + n)])
-                d = deps + [pl[book + st[1]]]
-                made[b].append(V(d, vec.tensor_copy, o, i) if st[2] == "v" else S(d, act, o, i, FN.Copy))
-                continue
-            tk = V(made[b], vec.quantize_mx, cc[:, 128 * a:128 * (a + n)], cs[:, 128 * a:128 * (a + n)], gt[:, 512 * a:512 * (a + n)])
-            send([tk], name % b, [([group[k]], u8(cc, 128 * k, 128 * (k + 1)), u8(kc, 128 * k, 128 * (k + 1))) for k in range(a, a + n)])
-            send([tk], name % b, [([group[k]], cs[:, 128 * k:128 * (k + 1)], ks[:, 128 * k:128 * (k + 1)]) for k in range(a, a + n)])
+        slot = list(range(n)) if no == "1" else [place] * n
+        tk = [mm(banks[i], K, rc, rs, 128 * q, qc, qs, at, [(name % q, landed(sent, i))]) for i, q in enumerate(group)]
+        block = [(2 * int(no) - 2 if z == 0 else 3 + int(no), a, m) for z, (a, m) in enumerate(cuts(groups))]
+        where = [32 * z + 4 * (i - a) for z, a, m in block for i in range(a, a + m)]
+        sc, sg, made, ready = {}, {}, [[] for _ in sizes], {}
+        for st in steps.split():
+            if st[0] == "s":
+                sc[int(st[1])] = scan(banks[int(st[1])], tk[int(st[1])])
+            elif st[0] == "n":
+                i = int(st[1])
+                sg[i] = sign(sc[i][0], 1, [sc[i][1], gz], T.gl[:, where[i]:where[i] + 1])
+            elif st == "t":
+                first = sc[0][0]
+                d = [S([s for _, s in sc.values()], act, mi[:, 0:2 * n:2], T.run[:, K * (first + 1) - 1:K * (first + n):K], FN.Copy)]
+                d += [S(list(sg.values()), act, mi[:, 2 * a + 1:2 * (a + m):2], T.gl[:, 32 * z:32 * z + 4 * m:4], FN.Identity,
+                        bias=float(K * me)) for z, a, m in block]
+                send(d, "as" + no, [([q], mi[:, 2 * i:2 * i + 2], sci[:, 4 * slot[i]:4 * slot[i] + 2]) for i, q in enumerate(group)])
+            elif st[0] == "L":
+                z, a, m = block[int(st[1])]
+                d = lists(z, m, of, 8 * a, [sg[i] for i in range(a, a + m)])
+                ready.update({i: d for i in range(a, a + m)})
+            elif st[0] == "g":
+                b, t = int(st[1]), int(st[2])
+                a, m = cuts(sizes)[b]
+                if len(st) > 4:
+                    a, m = a + int(st[4]), int(st[5])
+                o, i = gt[:, 512 * a + t:512 * (a + m):4], win[:, K * t:K * (t + 1)].indirect(of[:, 8 * a:8 * (a + m)])
+                d = [x for k in range(a, a + m) for x in ready[k]] + [pl[no + st[2]]]
+                made[b].append(V(d, vec.tensor_copy, o, i) if st[3] == "v" else S(d, act, o, i, FN.Copy))
+            elif st[0] == "q":
+                b = int(st[1])
+                a, m = cuts(sizes)[b]
+                d = V(made[b], vec.quantize_mx, cc[:, 128 * a:128 * (a + m)], cs[:, 128 * a:128 * (a + m)], gt[:, 512 * a:512 * (a + m)])
+                back = "k%s%d" % (no, b)
+                send([d], back, [([group[k]], u8(cc, 128 * k, 128 * (k + 1)), u8(kc, 128 * slot[k], 128 * (slot[k] + 1)))
+                                 for k in range(a, a + m)])
+                send([d], back, [([group[k]], cs[:, 128 * k:128 * (k + 1)], ks[:, 128 * slot[k]:128 * (slot[k] + 1)])
+                                 for k in range(a, a + m)])
+            else:
+                aside[st]()
 
     def receive(b, banks, sizes, who, kc, ks, name, tab, w, base, tt):
         a, n = cuts(sizes)[b]
-        tk = [unpack(banks[t], t, 128 * n, kc, ks, 128 * a, (name % b, 2 * n * width(n))) for t in range(4)]
-        for t in range(4):
-            tt[t].append(evac(who[b][t], banks[t], 128 * n, tab, w * t + base + 128 * a, tk[t]))
+        if name[1] == "2":
+            a = min(place ^ k for k in range(a, a + n))
+        part = [(int(st[0]), st[1], a + int(st[2]), int(st[3])) if len(st) > 2 else (int(st[0]), st[1], a, n) for st in who[b]]
+        come = (name % b, 2 * n * width(n))
+        tk = [unpack(bk, t, 128 * m, kc, ks, 128 * i, come) for (t, _, i, m), bk in zip(part, banks)]
+        for (t, e, i, m), bk, d in zip(part, banks, tk):
+            tt[t].append(evac(e, bk, 128 * m, tab, w * t + base + 128 * i, d))
 
-    sg1 = search(in1, [0, 1, 2, 3, 5, 6, 7], T.xqc, T.xqs, T.q1c, T.q1s, 0, "ax%d", 0, T.mi1, T.sci1, "as1")
-    held("list1", EVEN)
-    _, l1 = lists(0, 7, T.of1, 0, sg1)
-    answer(in1, BACK1, STEPS1, T.of1, T.c1p, "1", T.gt1, T.s1c, T.s1s, T.k1c, T.k1s, "k1%d", l1)
-    planes("wait2")
-
-    def choose(sci, n, ch, pp, top, no, pos, deps):
+    def choose(sci, n, ch, pp, top, no, pos, deps, ordered=False):
         sc = sci[:, 0:4 * n:4]
         a = V(deps, vec.tensor_reduce, top, sc, X, A.max)
         b = V([a], vec.tensor_scalar, ch[:, 0:n], sc, top, BIG, A.is_lt, A.mult)
         c = V([b], vec.tensor_tensor, ch[:, 8:8 + n], ch[:, 0:n], sci[:, 1:4 * n:4], A.add)
+        if ordered:
+            f = V([b], vec.tensor_tensor, ch[:, 24:24 + n], ch[:, 0:n], pp[:, 0:n], A.add)
+            V([c], vec.tensor_reduce, no, ch[:, 8:8 + n], X, A.min)
+            return V([f], vec.tensor_reduce, pos, ch[:, 24:24 + n], X, A.min)
         d = V([c], vec.tensor_reduce, no, ch[:, 8:8 + n], X, A.min)
         e = V([d], vec.tensor_scalar, ch[:, 16:16 + n], ch[:, 8:8 + n], no, BIG, A.is_gt, A.mult)
         f = V([e], vec.tensor_tensor, ch[:, 24:24 + n], ch[:, 16:16 + n], pp[:, 0:n], A.add)
@@ -291,39 +328,54 @@ def rank_program(g, core, T, topo):
     def col(c):
         return T.gl[:, c:c + 1]
 
-    NO = 96
+    rows = []
+
+    def decide1():
+        rows.append(lists(1, 3, T.op1, 0, [choose(T.sci1, 8, T.ch1, T.pp1, col(40), col(36), col(32), [("as1", 7 * width(7)), gz, p1] + ow)]))
+
+    road("1", in1, [0, 1, 2, 3, 5, 6, 7], "ax%d", OUT1, T.q1c, T.q1s, 0, BACK1, LISTS1, STEPS1,
+         {"c": decide1, "h": lambda: held("list1", EVEN)})
+    planes("wait2")
     held("wait2", ODD)
-    c1 = choose(T.sci1, 8, T.ch1, T.pp1, col(NO + 8), col(NO), col(32), [("as1", 7 * width(7)), gz, p1] + ow)
-    _, lp1 = lists(1, 1, T.op1, 0, [c1])
+    lp1 = rows[0]
     for b in range(len(BACK1)):
-        receive(b, [EVEN, ODD][b % 2], BACK1, EVAC1, T.k1c, T.k1s, "k1%d", T.tab1, W1, K, t1)
+        receive(b, [EVEN, ODD + EVEN][b % 2], BACK1, EVAC1, T.k1c, T.k1s, "k1%d", T.tab1, W1, K, t1)
+    held("pick1", EVEN[1:])
     rr = [V(lp1 + [dx] + t1[t], vec.tensor_tensor, T.rt[:, t:512:4], T.tab1[:, W1 * t:W1 * (t + 1)].indirect(T.op1[:, 0:8]),
             T.xt[:, t:512:4], A.add) for t in range(4)]
     qr = V(rr, vec.quantize_mx, T.rqc[:, m0:m0 + 128], T.rqs[:, m0:m0 + 128], T.rt[:, :])
     spread(qr, "ar%d" % me, T.rqc, T.rqs, m0, m0 + 128, out2, OUT2)
     planes("wait3")
 
-    tk = [mm(EVEN[k], K, T.rqc, T.rqs, m0, T.q2c, T.q2s, K * k, [qr, q2, lent]) for k in range(4)]
-    lo = []
+    tk = [mm(ODD[k], K, T.rqc, T.rqs, m0, T.q2c, T.q2s, K * k, [qr, q2, lent]) for k in range(4)]
+    assert home == list(range(home[0], home[0] + 4))
+    ends = []
     for h in (0, 1):
-        _, s = scan(EVEN[2 * h], tk[2 * h])
-        k, s = scan(EVEN[2 * h + 1], tk[2 * h + 1], s)
-        n = sign(k, 2, [s], T.ix[:, h:h + 1])
-        lo += [S([s], act, T.sci2[:, 16 + 4 * h:17 + 4 * h], last(k), FN.Copy),
-               S([n], act, T.sci2[:, 17 + 4 * h:18 + 4 * h], T.ix[:, h:h + 1], FN.Identity, bias=float(K * home[2 * h])),
-               S([n], act, T.pp2[:, 4 + h:5 + h], T.ix[:, h:h + 1], FN.Identity, bias=float(2 * K * h))]
+        _, s = scan(ODD[2 * h], tk[2 * h])
+        ends.append(scan(ODD[2 * h + 1], tk[2 * h + 1], s))
+    (ka, sa), (kb, sb_) = ends
+    na = sign(ka, 2, [sa], T.ix[:, 0:1])
+    na = S([na], act, T.pp2[:, 4:5], T.ix[:, 0:1], FN.Identity, bias=float(at_held))
     held("wait3", ODD)
-    sg2 = search(in2, ODD, T.rqc, T.rqs, T.q2c, T.q2s, h0, "ar%d", 2, T.mi2, T.sci2, "as2")
-    held("list2", EVEN)
-    _, l2 = lists(2, 4, T.of2, 0, sg2)
-    answer(in2, BACK2, STEPS2, T.of2, T.c2p, "2", T.gt2, T.s2c, T.s2s, T.k2c, T.k2s, "k2%d", l2)
+    lo = []
 
-    held("wait4", ODD)
-    c2 = choose(T.sci2, 6, T.ch2, T.pp2, col(NO + 12), col(NO + 4), col(NO + 16), [("as2", 4 * width(4)), p2] + lo)
-    nt, lp2 = lists(3, 5, T.op2, 4, [c2])
-    D("y", [nt], "no", T.no[:, :], T.wl[0:16, 12:14, :])
+    def settle():
+        lo.append(sign(kb, 2, [sb_], T.ix[:, 1:2]))
+
+    def settle2():
+        nc = S(lo, act, T.pp2[:, 5:6], T.ix[:, 1:2], FN.Identity, bias=float(at_held + 2 * K))
+        lo.append(S([sa, sb_], act, T.sci2[:, 16:24:4], T.run[:, K * (ka + 1) - 1:K * (kb + 1):2 * K], FN.Copy))
+        lo.append(S([na, nc], act, T.sci2[:, 17:24:4], T.pp2[:, 4:6], FN.Identity, bias=float(K * home[0] - at_held)))
+
+    def decide2():
+        rows.append(lists(3, 3, T.op2, 0, [choose(T.sci2, 6, T.ch2, T.pp2, col(104), col(100), col(96), [("as2", 4 * width(4)), p2] + lo, True)]))
+
+    road("2", in2, EVEN, "ar%d", OUT2, T.q2c, T.q2s, h0, BACK2, LISTS2, STEPS2,
+         {"c": decide2, "h": lambda: held("list2", ODD), "b": settle, "d": settle2})
+    lp2 = rows[1]
+    held("wait4", EVEN)
     for b in range(len(BACK2)):
-        receive(b, [EVEN, ODD][b % 2], BACK2, EVAC2, T.k2c, T.k2s, "k2%d", T.tab2, W2, 4 * K, t2)
+        receive(b, [ODD + EVEN, EVEN + ODD][b % 2], BACK2, EVAC2, T.k2c, T.k2s, "k2%d", T.tab2, W2, at_road, t2)
     for a, n in cuts(STORE):
         yy = [V(lp2 + rr + t2[t], vec.tensor_tensor, T.yt[:, 64 * a + t:64 * (a + n):4],
                 T.tab2[:, W2 * t:W2 * (t + 1)].indirect(T.op2[:, a:a + n]), T.rt[:, 64 * a + t:64 * (a + n):4], A.add) for t in range(4)]

@@ -7,16 +7,15 @@ W2 = 4 * K + 4 * 128
 BIG = 1000000.0
 LOW = -9.0e29
 
-OUT1, OUT2 = [("s", 0, 7, (0, 2)), ("c", 0, 2, (1, 2)), ("c", 2, 7, (0, 1))], [("s", 0, 4, (0, 1)), ("c", 0, 4, (0, 1))]
+OUT1, OUT2 = [("s", 0, 4, (0, 2)), ("c", 0, 1, (1, 2)), ("c", 1, 7, (0, 1)), ("s", 4, 7, (0, 1))], [("s", 0, 4, (0, 1)), ("c", 0, 4, (0, 1))]
 BACK1, BACK2 = [4, 3], [2, 2]
-LISTS1 = [7]
-LISTS2 = [4]
-STEPS1 = "s0 s1 s2 s3 s4 s5 s6 n0 n1 n2 n3 n4 n5 n6 t h L0 g00v g02s g01v g03s q0 g11s g12s g10v g13v q1 c"
-STEPS2 = "s0 s1 s2 s3 n0 n1 n2 n3 t b h L0 g00v g02s g01v g03s q0 g11s g12s d g10v g13v q1 c"
-EVAC1, EVAC2 = [["0v", "1s", "2s", "3s"], ["0v", "1s", "2v02", "2s21", "3s"]], [["0v", "1s", "2s", "3s"], ["0v", "1s", "2s", "3s"]]
-HELD = {"first": ["a0s", "a1s", "a2v", "a3v"], "early": ["01s"], "list1": ["02v", "03s", "00s"], "wait2": ["10s", "11s", "12s", "13s", "20s"], "pick1": ["21s", "22s", "23s"], "wait3": ["30s"], "list2": ["31v"], "wait4": ["32s", "33s"]}
-PLANES = {"early": ["13s"], "lent": ["10g", "11g", "12g"], "wait2": ["20g", "21g"], "wait3": ["22g", "23g"]}
+STEPS1 = "s s s s n n n n s s l0 s n n n l0 l0 l0 t l1 g01s g00v02 l1 g02s g00v22 l1 g03v02 l1 g03v21 g03s31 q0 g11s g12s g10v c g13s02 g13v21 c q1"
+STEPS2 = "s s n n s s l0 n n a l0 l0 l0 t b d l1 g01s g00v01 l1 g02s g00v11 l1 g03v01 l1 g03v11 q0 g11s g12s g10v c g13s01 g13v11 c q1"
+EVAC1, EVAC2 = [["0v", "1s", "2v", "3s"], ["0v", "1s", "2v02", "2s21", "3s"]], [["0s", "1s", "2s", "3s"], ["0v", "1s", "2s", "3s"]]
+HELD = {"first": ["a0s", "a1s", "a2v", "a3v"], "early": ["01s"], "wait2": ["02s", "03s", "00s", "10s", "11s"], "pick1": ["12s", "13s", "20s", "21s"], "sent": ["22v"], "wait3": ["23s"], "wait4": ["30s", "31s", "32s", "33s"]}
+PLANES = {"early": ["13s", "12s"], "lent": ["10g", "11g"], "wait2": ["20g", "21g"], "wait3": ["22g", "23g"]}
 STORE = [8]
+LOCAL = [0, 1, 2]
 
 F, B, C8, U8, I32, U16 = "float32", "bfloat16", "float8_e4m3fn_x4", "uint8", "int32", "uint16"
 
@@ -37,7 +36,7 @@ SCRATCH = {
     "s1c": sb(896, C8), "s1s": sb(896, U8), "s2c": sb(512, C8), "s2s": sb(512, U8),
     "k1c": sb(896, C8), "k1s": sb(896, U8), "k2c": sb(512, C8), "k2s": sb(512, U8),
     "sci1": sb(32, F), "sci2": sb(24, F), "tab1": sb(4 * W1, F), "tab2": sb(4 * W2, F),
-    "pp1": sb(8, F), "pp2": sb(6, F), "ix": sb(2, F), "ch1": sb(32, F), "ch2": sb(32, F),
+    "pp0": sb(7, F), "pp1": sb(8, F), "pp2": sb(6, F), "ix": sb(3, F), "ch1": sb(32, F), "ch2": sb(32, F),
     "rt": sb(512, B), "yt": sb(512, F),
 }
 for _b in range(8):
@@ -65,6 +64,9 @@ def rank_program(g, core, T, topo):
     near_out, near_in = [turn(home, k) for k in (1, 2, 3)], [turn(home, -k) for k in (1, 2, 3)]
     out1, in1 = out2 + near_out, in2 + near_in
     at_held, at_road = (0, 4 * K) if home[0] < far[0] else (4 * 128, 0)
+    cols2 = [at_road + 128 * k for k in range(4)]
+    at_own = 128 * me
+    cols1 = [128 * q + (K - 128) * (q > me) for q in far + [q for q in home if q != me]]
     sem = T.sem
     queue = {"v": g.vector, "s": g.scalar, "t": g.tensor, "g": g, "y": g.sync}
     count, seen, local, total = {}, {}, [0], {}
@@ -153,8 +155,8 @@ def rank_program(g, core, T, topo):
     def unpack(b, t, n, qc, qs, a, dep):
         return mm(b, n, T.eqc, T.eqs, 128 * t, qc, qs, a, [dep, qe[t]])
 
-    def evac(qn, b, n, tab, a, dep):
-        o, i = tab[:, a:a + n], bank[b][:, 0:n]
+    def evac(qn, b, n, tab, a, dep, at=0):
+        o, i = tab[:, a:a + n], bank[b][:, at:at + n]
         if qn == "v":
             tk = V([dep], vec.tensor_scalar, o, i, -1.0, None, A.mult)
         else:
@@ -168,46 +170,52 @@ def rank_program(g, core, T, topo):
 
     o1 = V([], vec.memset, T.ones[:, :], 1.0)
     i1 = G([o1], g.affine_select, T.ident[:, :], T.ones[:, 0:128], [[-1, 128]], A.is_equal, 0.0, 0, 1)
-    p1 = G([], g.iota, T.pp1[:, 0:7], [[128, 7]], K, 1, allow_small_or_imprecise_dtypes=True)
-    p2 = G([], g.iota, T.pp2[:, 0:4], [[128, 4]], at_road, 1, allow_small_or_imprecise_dtypes=True)
-    gz = G([], g.iota, T.gl[:, 0:128], [[0, 128]], 0, 0, allow_small_or_imprecise_dtypes=True)
+    p0 = G([], g.iota, T.pp0[:, :], [[128, 7]], 0, 1, allow_small_or_imprecise_dtypes=True)
+    runs = [(0, 4), (4, 4 + place), (4 + place, 7)]
+    p1 = [S([p0], act, T.pp1[:, a:b], T.pp0[:, a:b], FN.Identity, bias=float(cols1[a] - 128 * a)) for a, b in runs if a < b]
+    p2 = S([p0], act, T.pp2[:, 0:4], T.pp0[:, 0:4], FN.Identity, bias=float(at_road))
     ez = V([], vec.memset, T.et[:, :], 0.0)
+    gz = V([], vec.memset, T.gl[:, :], 0.0)
     ec = V([i1, ez], vec.tensor_copy, T.et[:, 3:515:4], T.ident[:, :])
-    qe = [V([ec], vec.quantize_mx, T.eqc[:, 128 * b:128 * (b + 1)], T.eqs[:, 128 * b:128 * (b + 1)], T.et[:, 3 - b:515 - b])
-          for b in range(4)]
 
     m0 = 128 * me
     qx = V([dx], vec.quantize_mx, T.xqc[:, m0:m0 + 128], T.xqs[:, m0:m0 + 128], T.xt[:, :])
     spread(qx, "ax%d" % me, T.xqc, T.xqs, m0, m0 + 128, out1, OUT1)
-
-    score_no = [0]
+    qe = [V([ec], vec.quantize_mx, T.eqc[:, 128 * b:128 * (b + 1)], T.eqs[:, 128 * b:128 * (b + 1)], T.et[:, 3 - b:515 - b])
+          for b in range(4)]
 
     def last(k):
         return T.run[:, K * (k + 1) - 1:K * (k + 1)]
 
-    def scan(b, dep, on=None):
-        k = score_no[0]
-        score_no[0] += 1
+    def scan(k, b, dep, on=None):
         tk = V([dep, o1] + ([on] if on else []), vec.tensor_tensor_scan, T.run[:, K * k:K * (k + 1)], bank[b][:, 0:K], T.ones[:, :],
                last(k - 1) if on else LOW, A.max, A.mult)
         free[b] = [tk]
-        return k, tk
+        return tk
 
     def sign(k, n, deps, acc):
         a, b = K * (k + 1 - n), K * (k + 1)
         return S(deps, act, T.junk[:, a:b], T.run[:, a:b], FN.Sign, bias=last(k), scale=-1.0, accum_out=acc)
 
-    def lists(z, n, of, at, deps):
+    def lists(z, n, of, at, deps, done):
         gl, wl, ol = 32 * z, 4 * z, 64 * z
         a = [V(deps + [gz], vec.tensor_copy, T.gl[0:32, gl + c:gl + 4 * n:4], T.gl[32 * c:32 * (c + 1), gl:gl + 4 * n:4])
              for c in (1, 2, 3)]
+        yield
         b = [V(a, vec.transpose, T.wl[0:32, wl + 2 * e:wl + 2 * e + 2, :], T.gl[0:32, gl:gl + 32]) for e in (0, 1)]
+        yield
         d = [V(b, vec.transpose, T.ol[0:32, ol + h:ol + 64:2], T.wl[0:32, wl + h:wl + 4:2, :]) for h in (0, 1)]
         if z in (1, 3):
             for c in (0, 1):
                 D("y", b, "no", T.no[z // 2 + 2 * c, :], T.wl[4 + 4 * c:8 + 4 * c, wl:wl + 2, :])
             n = 1
-        return [V(d, vec.tensor_copy, of[32 * c:32 * (c + 1), at:at + 8 * n], T.ol[0:32, ol:ol + 8 * n]) for c in range(4)]
+        yield
+        done.extend(V(d, vec.tensor_copy, of[32 * c:32 * (c + 1), at:at + 8 * n], T.ol[0:32, ol:ol + 8 * n]) for c in range(4))
+        yield
+
+    def finish(steps):
+        for _ in steps:
+            pass
 
     pl = {}
 
@@ -223,6 +231,7 @@ def rank_program(g, core, T, topo):
 
     t1 = [[], [], [], []]
     t2 = [[], [], [], []]
+    late = []
     lent = ("ac", 3 * 2 * width(1))
 
     def held(slot, banks):
@@ -232,11 +241,14 @@ def rank_program(g, core, T, topo):
             for st, b in zip(todo[a:a + len(banks)], banks):
                 t = int(st[1])
                 if st[0] == "a":
-                    part.append((t1[t], st[2], b, T.tab1, W1 * t, unpack(b, t, K, T.q1c, T.q1s, 0, q1)))
+                    part.append((t1[t], st[2], b, T.tab1, W1 * t + at_own, unpack(b, t, K, T.q1c, T.q1s, 0, q1)))
                 else:
                     k = (place + int(st[0])) % 4
                     part.append((t2[t], st[2], b, T.tab2, W2 * t + at_held + K * k,
                                  unpack(b, t, K, T.q2c, T.q2s, K * k, q2 if k == place else lent)))
+            if slot == "sent":
+                late.extend(part)
+                continue
             for tt, who, b, tab, at, tk in part:
                 tt.append(evac(who, b, K, tab, at, tk))
 
@@ -248,46 +260,45 @@ def rank_program(g, core, T, topo):
     send([q2], "ac", [(near_out, u8(T.q2c, h0, h0 + K), u8(T.q2c, h0, h0 + K))])
     send([q2], "ac", [(near_out, T.q2s[:, h0:h0 + K], T.q2s[:, h0:h0 + K])])
     planes("lent")
-    k0, s0 = scan(4, so)
+    s0 = scan(0, 4, so)
     held("first", [0, 1, 2, 3])
-    n0 = sign(k0, 1, [s0], T.pp1[:, 7:8])
-    ow = [n0, S([s0], act, T.sci1[:, 28:29], last(k0), FN.Copy),
-          S([n0], act, T.sci1[:, 29:30], T.pp1[:, 7:8], FN.Identity, bias=float(K * me))]
+    n0 = sign(0, 1, [s0], T.ix[:, 2:3])
+    ow = [S([s0], act, T.sci1[:, 28:29], last(0), FN.Copy),
+          S([n0], act, T.sci1[:, 29:30], T.ix[:, 2:3], FN.Identity, bias=float(K * me)),
+          S([n0], act, T.pp1[:, 7:8], T.ix[:, 2:3], FN.Identity, bias=float(at_own))]
     held("early", [5, 6, 7, 4])
 
-    def road(no, group, banks, name, sent, qc, qs, at, sizes, groups, steps, aside):
+    def road(no, group, banks, first, name, sent, qc, qs, at, sizes, steps, aside):
         rc, rs = (T.xqc, T.xqs) if no == "1" else (T.rqc, T.rqs)
         mi, sci, of, win, gt = T["mi" + no], T["sci" + no], T["of" + no], T["c%sp" % no], T["gt" + no]
         cc, cs, kc, ks = T["s%sc" % no], T["s%ss" % no], T["k%sc" % no], T["k%ss" % no]
         n = len(group)
-        slot = list(range(n)) if no == "1" else [place] * n
+        block = [(32 * z, a, m) for z, (a, m) in zip({"1": (0, 4), "2": (2, 5)}[no], cuts(sizes))]
+        index = [T.gl[:, at_ + 4 * i:at_ + 4 * i + 1] for at_, a, m in block for i in range(m)]
+        slot = [place if q in far else 4 + place - (place > home.index(q)) for q in group]
         tk = [mm(banks[i], K, rc, rs, 128 * q, qc, qs, at, [(name % q, landed(sent, i))]) for i, q in enumerate(group)]
-        block = [(2 * int(no) - 2 if z == 0 else 3 + int(no), a, m) for z, (a, m) in enumerate(cuts(groups))]
-        where = [32 * z + 4 * (i - a) for z, a, m in block for i in range(a, a + m)]
-        sc, sg, made, ready = {}, {}, [[] for _ in sizes], {}
+        sc, sg, made, ready = [], [[] for _ in sizes], [[] for _ in sizes], [[] for _ in sizes]
+        turns = [lists(at_ // 32, m, of, 8 * a, sg[b], ready[b]) for b, (at_, a, m) in enumerate(block)]
         for st in steps.split():
-            if st[0] == "s":
-                sc[int(st[1])] = scan(banks[int(st[1])], tk[int(st[1])])
-            elif st[0] == "n":
-                i = int(st[1])
-                sg[i] = sign(sc[i][0], 1, [sc[i][1], gz], T.gl[:, where[i]:where[i] + 1])
+            if st == "s":
+                sc.append(scan(first + len(sc), banks[len(sc)], tk[len(sc)]))
+            elif st == "n":
+                i = sum(map(len, sg))
+                sg[int(i >= sizes[0])].append(sign(first + i, 1, [sc[i], gz], index[i]))
             elif st == "t":
-                first = sc[0][0]
-                d = [S([s for _, s in sc.values()], act, mi[:, 0:2 * n:2], T.run[:, K * (first + 1) - 1:K * (first + n):K], FN.Copy)]
-                d += [S(list(sg.values()), act, mi[:, 2 * a + 1:2 * (a + m):2], T.gl[:, 32 * z:32 * z + 4 * m:4], FN.Identity,
-                        bias=float(K * me)) for z, a, m in block]
+                d = [S(sc, act, mi[:, 0:2 * n:2], T.run[:, K * (first + 1) - 1:K * (first + n):K], FN.Copy)]
+                d += [S(sg[b], act, mi[:, 2 * a + 1:2 * (a + m):2], T.gl[:, at_:at_ + 4 * m:4], FN.Identity, bias=float(K * me))
+                      for b, (at_, a, m) in enumerate(block)]
                 send(d, "as" + no, [([q], mi[:, 2 * i:2 * i + 2], sci[:, 4 * slot[i]:4 * slot[i] + 2]) for i, q in enumerate(group)])
-            elif st[0] == "L":
-                z, a, m = block[int(st[1])]
-                d = lists(z, m, of, 8 * a, [sg[i] for i in range(a, a + m)])
-                ready.update({i: d for i in range(a, a + m)})
+            elif st[0] == "l":
+                next(turns[int(st[1])])
             elif st[0] == "g":
                 b, t = int(st[1]), int(st[2])
                 a, m = cuts(sizes)[b]
                 if len(st) > 4:
                     a, m = a + int(st[4]), int(st[5])
                 o, i = gt[:, 512 * a + t:512 * (a + m):4], win[:, K * t:K * (t + 1)].indirect(of[:, 8 * a:8 * (a + m)])
-                d = [x for k in range(a, a + m) for x in ready[k]] + [pl[no + st[2]]]
+                d = ready[b] + [pl[no + st[2]]]
                 made[b].append(V(d, vec.tensor_copy, o, i) if st[3] == "v" else S(d, act, o, i, FN.Copy))
             elif st[0] == "q":
                 b = int(st[1])
@@ -301,46 +312,44 @@ def rank_program(g, core, T, topo):
             else:
                 aside[st]()
 
-    def receive(b, banks, sizes, who, kc, ks, name, tab, w, base, tt):
+    def receive(b, banks, sizes, who, kc, ks, name, tab, w, cols, tt):
         a, n = cuts(sizes)[b]
-        if name[1] == "2":
+        if a < 4:
             a = min(place ^ k for k in range(a, a + n))
         part = [(int(st[0]), st[1], a + int(st[2]), int(st[3])) if len(st) > 2 else (int(st[0]), st[1], a, n) for st in who[b]]
         come = (name % b, 2 * n * width(n))
         tk = [unpack(bk, t, 128 * m, kc, ks, 128 * i, come) for (t, _, i, m), bk in zip(part, banks)]
         for (t, e, i, m), bk, d in zip(part, banks, tk):
-            tt[t].append(evac(e, bk, 128 * m, tab, w * t + base + 128 * i, d))
+            cut = [k for k in range(i, i + m) if k == i or cols[k] != cols[k - 1] + 128] + [i + m]
+            for u, v in zip(cut, cut[1:]):
+                tt[t].append(evac(e, bk, 128 * (v - u), tab, w * t + cols[u], d, 128 * (u - i)))
 
-    def choose(sci, n, ch, pp, top, no, pos, deps, ordered=False):
+    def decide(z, sci, n, ch, pp, of, deps, done):
+        pos, no, top = [T.gl[:, 32 * z + c:32 * z + c + 1] for c in (0, 4, 8)]
         sc = sci[:, 0:4 * n:4]
         a = V(deps, vec.tensor_reduce, top, sc, X, A.max)
+        yield
         b = V([a], vec.tensor_scalar, ch[:, 0:n], sc, top, BIG, A.is_lt, A.mult)
-        c = V([b], vec.tensor_tensor, ch[:, 8:8 + n], ch[:, 0:n], sci[:, 1:4 * n:4], A.add)
-        if ordered:
-            f = V([b], vec.tensor_tensor, ch[:, 24:24 + n], ch[:, 0:n], pp[:, 0:n], A.add)
-            V([c], vec.tensor_reduce, no, ch[:, 8:8 + n], X, A.min)
-            return V([f], vec.tensor_reduce, pos, ch[:, 24:24 + n], X, A.min)
-        d = V([c], vec.tensor_reduce, no, ch[:, 8:8 + n], X, A.min)
-        e = V([d], vec.tensor_scalar, ch[:, 16:16 + n], ch[:, 8:8 + n], no, BIG, A.is_gt, A.mult)
-        f = V([e], vec.tensor_tensor, ch[:, 24:24 + n], ch[:, 16:16 + n], pp[:, 0:n], A.add)
-        return V([f], vec.tensor_reduce, pos, ch[:, 24:24 + n], X, A.min)
+        yield
+        c = [V([b], vec.tensor_tensor, ch[:, 8:8 + n], ch[:, 0:n], sci[:, 1:4 * n:4], A.add),
+             V([b], vec.tensor_tensor, ch[:, 16:16 + n], ch[:, 0:n], pp[:, 0:n], A.add)]
+        yield
+        d = [V(c[:1], vec.tensor_reduce, no, ch[:, 8:8 + n], X, A.min), V(c, vec.tensor_reduce, pos, ch[:, 16:16 + n], X, A.min)]
+        yield
+        for _ in lists(z, 3, of, 0, d, done):
+            yield
 
-    def col(c):
-        return T.gl[:, c:c + 1]
-
-    rows = []
-
-    def decide1():
-        rows.append(lists(1, 3, T.op1, 0, [choose(T.sci1, 8, T.ch1, T.pp1, col(40), col(36), col(32), [("as1", 7 * width(7)), gz, p1] + ow)]))
-
-    road("1", in1, [0, 1, 2, 3, 5, 6, 7], "ax%d", OUT1, T.q1c, T.q1s, 0, BACK1, LISTS1, STEPS1,
-         {"c": decide1, "h": lambda: held("list1", EVEN)})
+    lp1, lp2 = [], []
+    steps1 = decide(1, T.sci1, 8, T.ch1, T.pp1, T.op1, [("as1", 7 * width(7)), gz] + p1 + ow, lp1)
+    road("1", in1, [0, 1, 2, 3, 5, 6, 7], 1, "ax%d", OUT1, T.q1c, T.q1s, 0, BACK1, STEPS1,
+         {"c": lambda: next(steps1), "h": lambda: held("list1", EVEN)})
     planes("wait2")
     held("wait2", ODD)
-    lp1 = rows[0]
+    finish(steps1)
     for b in range(len(BACK1)):
-        receive(b, [EVEN, ODD + EVEN][b % 2], BACK1, EVAC1, T.k1c, T.k1s, "k1%d", T.tab1, W1, K, t1)
+        receive(b, [EVEN, ODD + EVEN][b % 2], BACK1, EVAC1, T.k1c, T.k1s, "k1%d", T.tab1, W1, cols1, t1)
     held("pick1", EVEN[1:])
+    held("sent", EVEN[:1])
     rr = [V(lp1 + [dx] + t1[t], vec.tensor_tensor, T.rt[:, t:512:4], T.tab1[:, W1 * t:W1 * (t + 1)].indirect(T.op1[:, 0:8]),
             T.xt[:, t:512:4], A.add) for t in range(4)]
     qr = V(rr, vec.quantize_mx, T.rqc[:, m0:m0 + 128], T.rqs[:, m0:m0 + 128], T.rt[:, :])
@@ -349,33 +358,44 @@ def rank_program(g, core, T, topo):
 
     tk = [mm(ODD[k], K, T.rqc, T.rqs, m0, T.q2c, T.q2s, K * k, [qr, q2, lent]) for k in range(4)]
     assert home == list(range(home[0], home[0] + 4))
-    ends = []
-    for h in (0, 1):
-        _, s = scan(ODD[2 * h], tk[2 * h])
-        ends.append(scan(ODD[2 * h + 1], tk[2 * h + 1], s))
-    (ka, sa), (kb, sb_) = ends
-    na = sign(ka, 2, [sa], T.ix[:, 0:1])
-    na = S([na], act, T.pp2[:, 4:5], T.ix[:, 0:1], FN.Identity, bias=float(at_held))
-    held("wait3", ODD)
+    ka, kb = 9, 11
+    done = {}
+
+    def local_scan(k):
+        done[k] = scan(8 + k, ODD[k], tk[k], done[k - 1] if k % 2 else None)
+
+    for k in LOCAL:
+        local_scan(k)
+        for tt, who, b, tab, at, d in late:
+            tt.append(evac(who, b, K, tab, at, d))
+        late.clear()
+    held("wait3", EVEN[1:])
+    na = sign(ka, 2, [done[1]], T.ix[:, 0:1])
     lo = []
 
+    def rest():
+        for k in range(4):
+            if k not in done:
+                local_scan(k)
+
     def settle():
-        lo.append(sign(kb, 2, [sb_], T.ix[:, 1:2]))
+        lo.append(sign(kb, 2, [done[3]], T.ix[:, 1:2]))
 
     def settle2():
-        nc = S(lo, act, T.pp2[:, 5:6], T.ix[:, 1:2], FN.Identity, bias=float(at_held + 2 * K))
-        lo.append(S([sa, sb_], act, T.sci2[:, 16:24:4], T.run[:, K * (ka + 1) - 1:K * (kb + 1):2 * K], FN.Copy))
-        lo.append(S([na, nc], act, T.sci2[:, 17:24:4], T.pp2[:, 4:6], FN.Identity, bias=float(K * home[0] - at_held)))
+        nb = lo[-1]
+        lo.append(S([done[1], done[3]], act, T.sci2[:, 16:24:4], T.run[:, K * (ka + 1) - 1:K * (kb + 1):2 * K], FN.Copy))
+        for h, d in enumerate((na, nb)):
+            lo.append(S([d], act, T.pp2[:, 4 + h:5 + h], T.ix[:, h:h + 1], FN.Identity, bias=float(at_held + 2 * K * h)))
+            lo.append(S([d], act, T.sci2[:, 17 + 4 * h:18 + 4 * h], T.ix[:, h:h + 1], FN.Identity, bias=float(K * home[2 * h])))
 
-    def decide2():
-        rows.append(lists(3, 3, T.op2, 0, [choose(T.sci2, 6, T.ch2, T.pp2, col(104), col(100), col(96), [("as2", 4 * width(4)), p2] + lo, True)]))
-
-    road("2", in2, EVEN, "ar%d", OUT2, T.q2c, T.q2s, h0, BACK2, LISTS2, STEPS2,
-         {"c": decide2, "h": lambda: held("list2", ODD), "b": settle, "d": settle2})
-    lp2 = rows[1]
+    lo += [("as2", 4 * width(4)), p2]
+    steps2 = decide(3, T.sci2, 6, T.ch2, T.pp2, T.op2, lo, lp2)
+    road("2", in2, EVEN, 12, "ar%d", OUT2, T.q2c, T.q2s, h0, BACK2, STEPS2,
+         {"c": lambda: next(steps2), "h": lambda: held("list2", ODD), "a": rest, "b": settle, "d": settle2})
     held("wait4", EVEN)
+    finish(steps2)
     for b in range(len(BACK2)):
-        receive(b, [ODD + EVEN, EVEN + ODD][b % 2], BACK2, EVAC2, T.k2c, T.k2s, "k2%d", T.tab2, W2, at_road, t2)
+        receive(b, [ODD + EVEN, EVEN + ODD][b % 2], BACK2, EVAC2, T.k2c, T.k2s, "k2%d", T.tab2, W2, cols2, t2)
     for a, n in cuts(STORE):
         yy = [V(lp2 + rr + t2[t], vec.tensor_tensor, T.yt[:, 64 * a + t:64 * (a + n):4],
                 T.tab2[:, W2 * t:W2 * (t + 1)].indirect(T.op2[:, a:a + n]), T.rt[:, 64 * a + t:64 * (a + n):4], A.add) for t in range(4)]

from concourse.bass import DstId, RemoteDMATransfer
from concourse.mybir import dt, AluOpType, AxisListType, ActivationFunctionType

N, K = 8, 384
W1 = K + 7 * 128
W2 = 4 * K + 4 * 128
BIG = 1000000.0
LOW = -9.0e29

OUT1, OUT2 = [("s", 0, 4, (0, 2)), ("c", 0, 1, (1, 2)), ("c", 1, 7, (0, 1)), ("s", 4, 7, (0, 1))], [("s", 0, 4, (0, 1)), ("c", 0, 4, (0, 1))]
BACK1, BACK2 = [4, 3], [2, 2]
STEPS1 = "s s s s n n n n s s l0 s n n n l0 l0 l0 t l1 g01s g00v02 l1 g02s g00v22 l1 g03v02 l1 g03v21 g03s31 q0 g11s g12s g10v c g13s02 g13v21 c q1"
STEPS2 = "s s n n s s l0 n n a l0 l0 l0 t b d l1 g01s g00v01 l1 g02s g00v11 l1 g03v01 l1 g03v11 q0 g11s g12s g10v c g13s01 g13v11 c q1"
EVAC1, EVAC2 = [["0v", "1s", "2v", "3s"], ["0v", "1s", "2v02", "2s21", "3s"]], [["0s", "1s", "2s", "3s"], ["0v", "1s", "2s", "3s"]]
HELD = {"first": ["a0s", "a1s", "a2v", "a3v"], "early": ["01s"], "wait2": ["02s", "03s", "00s", "10s", "11s"], "pick1": ["12s", "13s", "20s", "21s"], "sent": ["22v"], "wait3": ["23s"], "wait4": ["30s", "31s", "32s", "33s"]}
PLANES = {"early": ["13s", "12s"], "lent": ["10g", "11g"], "wait2": ["20g", "21g"], "wait3": ["22g", "23g"]}
STORE = [8]
LOCAL = [0, 1, 2]

F, B, C8, U8, I32, U16 = "float32", "bfloat16", "float8_e4m3fn_x4", "uint8", "int32", "uint16"


def sb(n, d):
    return ("sbuf", [128, n], d)


SCRATCH = {
    "xt": sb(512, B), "c1t": sb(4 * K, B), "c2t": sb(4 * K, B), "c1p": sb(4 * K, B), "c2p": sb(4 * K, B),
    "ones": sb(K, B), "ident": sb(128, B), "et": sb(516, B), "eqc": sb(512, C8), "eqs": sb(512, U8),
    "xqc": sb(1024, C8), "xqs": sb(1024, U8), "rqc": sb(1024, C8), "rqs": sb(1024, U8),
    "q1c": sb(K, C8), "q1s": sb(K, U8), "q2c": sb(4 * K, C8), "q2s": sb(4 * K, U8),
    "run": sb(16 * K, F), "junk": sb(16 * K, B),
    "gl": sb(192, F), "wl": ("sbuf", [128, 24, 16], F), "ol": sb(384, F),
    "mi1": sb(16, F), "mi2": sb(8, F), "of1": sb(56, U16), "of2": sb(32, U16), "op1": sb(8, U16), "op2": sb(8, U16),
    "gt1": sb(7 * 512, B), "gt2": sb(4 * 512, B),
    "s1c": sb(896, C8), "s1s": sb(896, U8), "s2c": sb(512, C8), "s2s": sb(512, U8),
    "k1c": sb(896, C8), "k1s": sb(896, U8), "k2c": sb(512, C8), "k2s": sb(512, U8),
    "sci1": sb(32, F), "sci2": sb(24, F), "tab1": sb(4 * W1, F), "tab2": sb(4 * W2, F),
    "pp0": sb(7, F), "pp1": sb(8, F), "pp2": sb(6, F), "ix": sb(3, F), "ch1": sb(32, F), "ch2": sb(32, F),
    "rt": sb(512, B), "yt": sb(512, F),
}
for _b in range(8):
    SCRATCH["p%d" % _b] = ("psum", [128, 512], F)
SEMAPHORES = (["pv", "ps", "pt", "pg", "ls", "lx", "lc1", "lc2", "no", "yo", "ac", "as1", "as2"]
              + ["ax%d" % q for q in range(N)] + ["ar%d" % q for q in range(N)]
              + ["k1%d" % b for b in range(len(BACK1))] + ["k2%d" % b for b in range(len(BACK2))])


def rank_program(g, core, T, topo):
    me = T.rank_of(core)
    if me is None:
        return
    A, X, FN = AluOpType, AxisListType.X, ActivationFunctionType
    ranks = list(range(N))

    home = [q for q in ranks if topo.die(T.cores[q]) == topo.die(core)]
    far = [q for q in ranks if q not in home]
    place = home.index(me)

    def turn(group, k):
        return group[(place + k) % len(group)]

    out2 = in2 = [far[place ^ k] for k in range(4)]
    near_out, near_in = [turn(home, k) for k in (1, 2, 3)], [turn(home, -k) for k in (1, 2, 3)]
    out1, in1 = out2 + near_out, in2 + near_in
    at_held, at_road = (0, 4 * K) if home[0] < far[0] else (4 * 128, 0)
    cols2 = [at_road + 128 * k for k in range(4)]
    at_own = 128 * me
    cols1 = [128 * q + (K - 128) * (q > me) for q in far + [q for q in home if q != me]]
    sem = T.sem
    queue = {"v": g.vector, "s": g.scalar, "t": g.tensor, "g": g, "y": g.sync}
    count, seen, local, total = {}, {}, [0], {}

    def need(qn, deps):
        top = {}
        for s, v in deps:
            top[s] = max(top.get(s, 0), v)
        for s in sorted(top):
            if seen.get((qn, s), 0) < top[s]:
                queue[qn].wait_ge(sem[s], top[s])
                seen[(qn, s)] = top[s]

    def did(name, ins):
        ins.then_inc(sem[name], 1)
        count[name] = count.get(name, 0) + 1
        return (name, count[name])

    def V(deps, call, *a, **k):
        need("v", deps)
        return did("pv", call(*a, **k))

    def S(deps, call, *a, **k):
        need("s", deps)
        return did("ps", call(*a, **k))

    def G(deps, call, *a, **k):
        need("g", deps)
        return did("pg", call(*a, **k))

    def D(qn, deps, name, out, in_):
        need(qn, deps)
        queue[qn].dma_start(out, in_).then_inc(sem[name], 16)
        total[name] = total.get(name, 0) + 16
        return (name, total[name])

    vec, act = g.vector, g.scalar.activation
    engines = topo.engines(core, T.cores[(me + 1) % N])

    def width(n):
        k = 1
        while k < n:
            k *= 2
        return len(engines) // k

    def send(deps, name, items, part=(0, 1)):
        need("g", deps)
        per = width(len(items)) // part[1]
        step = len(engines) // per
        tr = []
        for k, (dst, s, d) in enumerate(items):
            mask = 0
            for e in engines[k + part[0]::step]:
                mask |= 1 << e
            ids = []
            for q in dst:
                rid, pid, _ = topo.addr(T.cores[q])
                ids.append(DstId(rid=rid, pnc=pid))
            tr.append(RemoteDMATransfer(dst_ids=ids, dma_engine_mask=mask, remote_sem=sem[name], srcs=[s], dsts=[d] * len(ids)))
            local[0] += per
        g.remote_dma_fused(tr, local_sem=sem.ls)

    def u8(t, a, b):
        return t[:, a:b].bitcast(dt.uint8)

    def cuts(sizes):
        return [(sum(sizes[:b]), n) for b, n in enumerate(sizes)]

    def spread(dep, name, qc, qs, a, b, dst, sizes):
        for kind, i, j, part in sizes:
            v = qs[:, a:b] if kind == "s" else u8(qc, a, b)
            send([dep], name, [(dst[i:j], v, v)], part)

    def landed(sizes, k):
        return sum(len(engines) // part[1] for _, i, j, part in sizes if i <= k < j)

    bank = [T["p%d" % b] for b in range(8)]
    free = [[] for _ in range(8)]
    EVEN, ODD = [4, 0, 1, 2], [3, 5, 6, 7]

    def mm(b, n, lc, lsc, la, rc, rsc, ra, deps):
        need("t", deps + free[b])
        return did("pt", g.tensor.matmul_mx(bank[b][:, 0:n], lc[:, la:la + 128], lsc[:, la:la + 128],
                                            rc[:, ra:ra + n], rsc[:, ra:ra + n], True, True))

    def unpack(b, t, n, qc, qs, a, dep):
        return mm(b, n, T.eqc, T.eqs, 128 * t, qc, qs, a, [dep, qe[t]])

    def evac(qn, b, n, tab, a, dep, at=0):
        o, i = tab[:, a:a + n], bank[b][:, at:at + n]
        if qn == "v":
            tk = V([dep], vec.tensor_scalar, o, i, -1.0, None, A.mult)
        else:
            tk = S([dep], act, o, i, FN.Copy, scale=-1.0)
        free[b] = [tk]
        return tk

    dx = D("y", [], "lx", T.xt[:, :], T.x[:, :])
    d1 = D("y", [], "lc1", T.c1t[:, :], T.c1[:, :])
    d2 = D("y", [], "lc2", T.c2t[:, :], T.c2[:, :])

    o1 = V([], vec.memset, T.ones[:, :], 1.0)
    i1 = G([o1], g.affine_select, T.ident[:, :], T.ones[:, 0:128], [[-1, 128]], A.is_equal, 0.0, 0, 1)
    p0 = G([], g.iota, T.pp0[:, :], [[128, 7]], 0, 1, allow_small_or_imprecise_dtypes=True)
    runs = [(0, 4), (4, 4 + place), (4 + place, 7)]
    p1 = [S([p0], act, T.pp1[:, a:b], T.pp0[:, a:b], FN.Identity, bias=float(cols1[a] - 128 * a)) for a, b in runs if a < b]
    p2 = S([p0], act, T.pp2[:, 0:4], T.pp0[:, 0:4], FN.Identity, bias=float(at_road))
    ez = V([], vec.memset, T.et[:, :], 0.0)
    gz = V([], vec.memset, T.gl[:, :], 0.0)
    ec = V([i1, ez], vec.tensor_copy, T.et[:, 3:515:4], T.ident[:, :])

    m0 = 128 * me
    qx = V([dx], vec.quantize_mx, T.xqc[:, m0:m0 + 128], T.xqs[:, m0:m0 + 128], T.xt[:, :])
    spread(qx, "ax%d" % me, T.xqc, T.xqs, m0, m0 + 128, out1, OUT1)
    qe = [V([ec], vec.quantize_mx, T.eqc[:, 128 * b:128 * (b + 1)], T.eqs[:, 128 * b:128 * (b + 1)], T.et[:, 3 - b:515 - b])
          for b in range(4)]

    def last(k):
        return T.run[:, K * (k + 1) - 1:K * (k + 1)]

    def scan(k, b, dep, on=None):
        tk = V([dep, o1] + ([on] if on else []), vec.tensor_tensor_scan, T.run[:, K * k:K * (k + 1)], bank[b][:, 0:K], T.ones[:, :],
               last(k - 1) if on else LOW, A.max, A.mult)
        free[b] = [tk]
        return tk

    def sign(k, n, deps, acc):
        a, b = K * (k + 1 - n), K * (k + 1)
        return S(deps, act, T.junk[:, a:b], T.run[:, a:b], FN.Sign, bias=last(k), scale=-1.0, accum_out=acc)

    def lists(z, n, of, at, deps, done):
        gl, wl, ol = 32 * z, 4 * z, 64 * z
        a = [V(deps + [gz], vec.tensor_copy, T.gl[0:32, gl + c:gl + 4 * n:4], T.gl[32 * c:32 * (c + 1), gl:gl + 4 * n:4])
             for c in (1, 2, 3)]
        yield
        b = [V(a, vec.transpose, T.wl[0:32, wl + 2 * e:wl + 2 * e + 2, :], T.gl[0:32, gl:gl + 32]) for e in (0, 1)]
        yield
        d = [V(b, vec.transpose, T.ol[0:32, ol + h:ol + 64:2], T.wl[0:32, wl + h:wl + 4:2, :]) for h in (0, 1)]
        if z in (1, 3):
            for c in (0, 1):
                D("y", b, "no", T.no[z // 2 + 2 * c, :], T.wl[4 + 4 * c:8 + 4 * c, wl:wl + 2, :])
            n = 1
        yield
        done.extend(V(d, vec.tensor_copy, of[32 * c:32 * (c + 1), at:at + 8 * n], T.ol[0:32, ol:ol + 8 * n]) for c in range(4))
        yield

    def finish(steps):
        for _ in steps:
            pass

    pl = {}

    def planes(slot):
        for st in PLANES[slot]:
            win, src, dep = (T.c1p, T.c1t, d1) if st[0] == "1" else (T.c2p, T.c2t, d2)
            t = int(st[1])
            o, i = win[:, K * t:K * (t + 1)], src[:, t:4 * K:4]
            if st[2] == "g":
                pl[st[:2]] = G([dep], g.affine_select, o, i, [[0, K]], A.is_ge, 0.0, 0, 0)
            else:
                pl[st[:2]] = V([dep], vec.tensor_copy, o, i) if st[2] == "v" else S([dep], act, o, i, FN.Copy)

    t1 = [[], [], [], []]
    t2 = [[], [], [], []]
    late = []
    lent = ("ac", 3 * 2 * width(1))

    def held(slot, banks):
        todo = HELD[slot]
        for a in range(0, len(todo), len(banks)):
            part = []
            for st, b in zip(todo[a:a + len(banks)], banks):
                t = int(st[1])
                if st[0] == "a":
                    part.append((t1[t], st[2], b, T.tab1, W1 * t + at_own, unpack(b, t, K, T.q1c, T.q1s, 0, q1)))
                else:
                    k = (place + int(st[0])) % 4
                    part.append((t2[t], st[2], b, T.tab2, W2 * t + at_held + K * k,
                                 unpack(b, t, K, T.q2c, T.q2s, K * k, q2 if k == place else lent)))
            if slot == "sent":
                late.extend(part)
                continue
            for tt, who, b, tab, at, tk in part:
                tt.append(evac(who, b, K, tab, at, tk))

    h0 = K * place
    q1 = V([d1], vec.quantize_mx, T.q1c[:, :], T.q1s[:, :], T.c1t[:, :])
    q2 = V([d2], vec.quantize_mx, T.q2c[:, h0:h0 + K], T.q2s[:, h0:h0 + K], T.c2t[:, :])
    so = mm(4, K, T.xqc, T.xqs, m0, T.q1c, T.q1s, 0, [qx, q1])
    planes("early")
    send([q2], "ac", [(near_out, u8(T.q2c, h0, h0 + K), u8(T.q2c, h0, h0 + K))])
    send([q2], "ac", [(near_out, T.q2s[:, h0:h0 + K], T.q2s[:, h0:h0 + K])])
    planes("lent")
    s0 = scan(0, 4, so)
    held("first", [0, 1, 2, 3])
    n0 = sign(0, 1, [s0], T.ix[:, 2:3])
    ow = [S([s0], act, T.sci1[:, 28:29], last(0), FN.Copy),
          S([n0], act, T.sci1[:, 29:30], T.ix[:, 2:3], FN.Identity, bias=float(K * me)),
          S([n0], act, T.pp1[:, 7:8], T.ix[:, 2:3], FN.Identity, bias=float(at_own))]
    held("early", [5, 6, 7, 4])

    def road(no, group, banks, first, name, sent, qc, qs, at, sizes, steps, aside):
        rc, rs = (T.xqc, T.xqs) if no == "1" else (T.rqc, T.rqs)
        mi, sci, of, win, gt = T["mi" + no], T["sci" + no], T["of" + no], T["c%sp" % no], T["gt" + no]
        cc, cs, kc, ks = T["s%sc" % no], T["s%ss" % no], T["k%sc" % no], T["k%ss" % no]
        n = len(group)
        block = [(32 * z, a, m) for z, (a, m) in zip({"1": (0, 4), "2": (2, 5)}[no], cuts(sizes))]
        index = [T.gl[:, at_ + 4 * i:at_ + 4 * i + 1] for at_, a, m in block for i in range(m)]
        slot = [place if q in far else 4 + place - (place > home.index(q)) for q in group]
        tk = [mm(banks[i], K, rc, rs, 128 * q, qc, qs, at, [(name % q, landed(sent, i))]) for i, q in enumerate(group)]
        sc, sg, made, ready = [], [[] for _ in sizes], [[] for _ in sizes], [[] for _ in sizes]
        turns = [lists(at_ // 32, m, of, 8 * a, sg[b], ready[b]) for b, (at_, a, m) in enumerate(block)]
        for st in steps.split():
            if st == "s":
                sc.append(scan(first + len(sc), banks[len(sc)], tk[len(sc)]))
            elif st == "n":
                i = sum(map(len, sg))
                sg[int(i >= sizes[0])].append(sign(first + i, 1, [sc[i], gz], index[i]))
            elif st == "t":
                d = [S(sc, act, mi[:, 0:2 * n:2], T.run[:, K * (first + 1) - 1:K * (first + n):K], FN.Copy)]
                d += [S(sg[b], act, mi[:, 2 * a + 1:2 * (a + m):2], T.gl[:, at_:at_ + 4 * m:4], FN.Identity, bias=float(K * me))
                      for b, (at_, a, m) in enumerate(block)]
                send(d, "as" + no, [([q], mi[:, 2 * i:2 * i + 2], sci[:, 4 * slot[i]:4 * slot[i] + 2]) for i, q in enumerate(group)])
            elif st[0] == "l":
                next(turns[int(st[1])])
            elif st[0] == "g":
                b, t = int(st[1]), int(st[2])
                a, m = cuts(sizes)[b]
                if len(st) > 4:
                    a, m = a + int(st[4]), int(st[5])
                o, i = gt[:, 512 * a + t:512 * (a + m):4], win[:, K * t:K * (t + 1)].indirect(of[:, 8 * a:8 * (a + m)])
                d = ready[b] + [pl[no + st[2]]]
                made[b].append(V(d, vec.tensor_copy, o, i) if st[3] == "v" else S(d, act, o, i, FN.Copy))
            elif st[0] == "q":
                b = int(st[1])
                a, m = cuts(sizes)[b]
                d = V(made[b], vec.quantize_mx, cc[:, 128 * a:128 * (a + m)], cs[:, 128 * a:128 * (a + m)], gt[:, 512 * a:512 * (a + m)])
                back = "k%s%d" % (no, b)
                send([d], back, [([group[k]], u8(cc, 128 * k, 128 * (k + 1)), u8(kc, 128 * slot[k], 128 * (slot[k] + 1)))
                                 for k in range(a, a + m)])
                send([d], back, [([group[k]], cs[:, 128 * k:128 * (k + 1)], ks[:, 128 * slot[k]:128 * (slot[k] + 1)])
                                 for k in range(a, a + m)])
            else:
                aside[st]()

    def receive(b, banks, sizes, who, kc, ks, name, tab, w, cols, tt):
        a, n = cuts(sizes)[b]
        if a < 4:
            a = min(place ^ k for k in range(a, a + n))
        part = [(int(st[0]), st[1], a + int(st[2]), int(st[3])) if len(st) > 2 else (int(st[0]), st[1], a, n) for st in who[b]]
        come = (name % b, 2 * n * width(n))
        tk = [unpack(bk, t, 128 * m, kc, ks, 128 * i, come) for (t, _, i, m), bk in zip(part, banks)]
        for (t, e, i, m), bk, d in zip(part, banks, tk):
            cut = [k for k in range(i, i + m) if k == i or cols[k] != cols[k - 1] + 128] + [i + m]
            for u, v in zip(cut, cut[1:]):
                tt[t].append(evac(e, bk, 128 * (v - u), tab, w * t + cols[u], d, 128 * (u - i)))

    def decide(z, sci, n, ch, pp, of, deps, done):
        pos, no, top = [T.gl[:, 32 * z + c:32 * z + c + 1] for c in (0, 4, 8)]
        sc = sci[:, 0:4 * n:4]
        a = V(deps, vec.tensor_reduce, top, sc, X, A.max)
        yield
        b = V([a], vec.tensor_scalar, ch[:, 0:n], sc, top, BIG, A.is_lt, A.mult)
        yield
        c = [V([b], vec.tensor_tensor, ch[:, 8:8 + n], ch[:, 0:n], sci[:, 1:4 * n:4], A.add),
             V([b], vec.tensor_tensor, ch[:, 16:16 + n], ch[:, 0:n], pp[:, 0:n], A.add)]
        yield
        d = [V(c[:1], vec.tensor_reduce, no, ch[:, 8:8 + n], X, A.min), V(c, vec.tensor_reduce, pos, ch[:, 16:16 + n], X, A.min)]
        yield
        for _ in lists(z, 3, of, 0, d, done):
            yield

    lp1, lp2 = [], []
    steps1 = decide(1, T.sci1, 8, T.ch1, T.pp1, T.op1, [("as1", 7 * width(7)), gz] + p1 + ow, lp1)
    road("1", in1, [0, 1, 2, 3, 5, 6, 7], 1, "ax%d", OUT1, T.q1c, T.q1s, 0, BACK1, STEPS1,
         {"c": lambda: next(steps1), "h": lambda: held("list1", EVEN)})
    planes("wait2")
    held("wait2", ODD)
    finish(steps1)
    for b in range(len(BACK1)):
        receive(b, [EVEN, ODD + EVEN][b % 2], BACK1, EVAC1, T.k1c, T.k1s, "k1%d", T.tab1, W1, cols1, t1)
    held("pick1", EVEN[1:])
    held("sent", EVEN[:1])
    rr = [V(lp1 + [dx] + t1[t], vec.tensor_tensor, T.rt[:, t:512:4], T.tab1[:, W1 * t:W1 * (t + 1)].indirect(T.op1[:, 0:8]),
            T.xt[:, t:512:4], A.add) for t in range(4)]
    qr = V(rr, vec.quantize_mx, T.rqc[:, m0:m0 + 128], T.rqs[:, m0:m0 + 128], T.rt[:, :])
    spread(qr, "ar%d" % me, T.rqc, T.rqs, m0, m0 + 128, out2, OUT2)
    planes("wait3")

    tk = [mm(ODD[k], K, T.rqc, T.rqs, m0, T.q2c, T.q2s, K * k, [qr, q2, lent]) for k in range(4)]
    assert home == list(range(home[0], home[0] + 4))
    ka, kb = 9, 11
    done = {}

    def local_scan(k):
        done[k] = scan(8 + k, ODD[k], tk[k], done[k - 1] if k % 2 else None)

    for k in LOCAL:
        local_scan(k)
        for tt, who, b, tab, at, d in late:
            tt.append(evac(who, b, K, tab, at, d))
        late.clear()
    held("wait3", EVEN[1:])
    na = sign(ka, 2, [done[1]], T.ix[:, 0:1])
    lo = []

    def rest():
        for k in range(4):
            if k not in done:
                local_scan(k)

    def settle():
        lo.append(sign(kb, 2, [done[3]], T.ix[:, 1:2]))

    def settle2():
        nb = lo[-1]
        lo.append(S([done[1], done[3]], act, T.sci2[:, 16:24:4], T.run[:, K * (ka + 1) - 1:K * (kb + 1):2 * K], FN.Copy))
        for h, d in enumerate((na, nb)):
            lo.append(S([d], act, T.pp2[:, 4 + h:5 + h], T.ix[:, h:h + 1], FN.Identity, bias=float(at_held + 2 * K * h)))
            lo.append(S([d], act, T.sci2[:, 17 + 4 * h:18 + 4 * h], T.ix[:, h:h + 1], FN.Identity, bias=float(K * home[2 * h])))

    lo += [("as2", 4 * width(4)), p2]
    steps2 = decide(3, T.sci2, 6, T.ch2, T.pp2, T.op2, lo, lp2)
    road("2", in2, EVEN, 12, "ar%d", OUT2, T.q2c, T.q2s, h0, BACK2, STEPS2,
         {"c": lambda: next(steps2), "h": lambda: held("list2", ODD), "a": rest, "b": settle, "d": settle2})
    held("wait4", EVEN)
    finish(steps2)
    for b in range(len(BACK2)):
        receive(b, [ODD + EVEN, EVEN + ODD][b % 2], BACK2, EVAC2, T.k2c, T.k2s, "k2%d", T.tab2, W2, cols2, t2)
    for a, n in cuts(STORE):
        yy = [V(lp2 + rr + t2[t], vec.tensor_tensor, T.yt[:, 64 * a + t:64 * (a + n):4],
                T.tab2[:, W2 * t:W2 * (t + 1)].indirect(T.op2[:, a:a + n]), T.rt[:, 64 * a + t:64 * (a + n):4], A.add) for t in range(4)]
        D("y", yy, "yo", T.y[:, 64 * a:64 * (a + n)], T.yt[:, 64 * a:64 * (a + n)])

    need("g", [(n, count[n]) for n in count] + [("ls", local[0])])
    need("y", [(n, total[n]) for n in total])
